import numpy as np
import ml_dtypes


def mxq(x, axis, fmt="e4m3"):
    dtype, down = {"e4m3": (ml_dtypes.float8_e4m3fn, 7), "e5m2": (ml_dtypes.float8_e5m2, 14)}[fmt]
    v = np.moveaxis(np.asarray(x, np.float32).astype(ml_dtypes.bfloat16).astype(np.float64), axis, -1)
    blocks = v.reshape(v.shape[:-1] + (-1, 32))
    amax = np.abs(blocks).max(-1, keepdims=True)
    byte = np.maximum(np.where(amax > 0, np.frexp(amax)[1] - 1 + 127, 0) - down, 1)
    scale = np.exp2(byte - 127.0)
    codes = (blocks / scale).astype(np.float32).astype(dtype).astype(np.float64)
    return np.moveaxis((codes * scale).reshape(v.shape), -1, axis)


WIDE = False


def mx_kscale(k):
    if not WIDE:
        return np.ones(k)
    levels = np.array([10, -10, 5, -5, 0])
    if k % 512:
        return np.exp2(np.random.permutation(np.resize(levels, k // 32))).repeat(32)
    a = np.empty((k // 512, 16))
    for p in range(k // 512):
        a[p, :8] = np.random.permutation(np.resize(levels, 8))
        for g in range(8):
            far = levels[np.abs(levels - a[p, g]) >= 10]
            a[p, g + 8] = far[np.random.randint(len(far))]
    return np.exp2(a.ravel()).repeat(32)


def f64(x):
    return np.asarray(x).astype(np.float64)


def striped(idx):
    return np.tile(idx.reshape(-1, 16).T, (8, 1)).astype(np.uint16)


def unstriped(offs):
    return offs[:16].T.reshape(-1).astype(np.int64)


K, T, D, S, V, R, N = 1024, 1024, 4, 512, 128, 8, 512


def setup_inputs():
    n = np.random.standard_normal
    s = mx_kscale(K)[:, None]
    return {
        "xT": (n((K, T)) * s).astype(np.float32),
        "w": (n((D, K, N)) / np.sqrt(D * K) / s[None]).astype(np.float32),
        "offs": striped(np.concatenate([R * np.arange(V) + np.random.randint(0, R, V) for _ in range(D)])),
    }


def reference(xT, w, offs):
    idx = unstriped(offs)
    xq = mxq(f64(xT)[:, idx], 0, "e4m3")
    wq = mxq(f64(w), 1, "e4m3")
    y = sum(wq[d].T @ xq[:, d * V:(d + 1) * V] for d in range(D))
    return y

@@ -1,0 +1,155 @@
+import concourse.mybir as mybir
+
+D, K, T, S, V, M = 4, 1024, 1024, 512, 128, 512
+FLOPS = 2 * K * M * S
+
+F32 = mybir.dt.float32
+BF16 = mybir.dt.bfloat16
+U32 = mybir.dt.uint32
+U16 = mybir.dt.uint16
+U8 = mybir.dt.uint8
+FP8X4 = mybir.dt.float8_e4m3fn_x4
+
+P = 128
+PACK = 4
+K_PASS = P * PACK
+PASSES = K // K_PASS
+M_TILE = 128
+ALIGN = 64
+
+LOADS = (
+    ("x", 0), ("w", 0), ("x", 1), ("w", 1), ("w", 2), ("w", 3, 0, 0, M), ("w", 3, 1, 0, 256), ("w", 3, 1, 256, 128), ("w", 3, 1, 384, 128),
+)
+X_HALF = T // 2
+X_SCALAR = 320
+
+
+def w_scalar(width):
+    return 288 * width // M if width == M else 96 * width // 256
+
+
+def interleave(nc, grouped, raw, scalar_columns):
+    def views(cols):
+        dst = grouped[:, cols, :].rearrange("p (c i) j -> p c j i", i=2)
+        src = raw[:, :, cols].rearrange("p j (c i) -> p c j i", i=2)
+        return dst, src
+
+    dst, src = views(slice(0, scalar_columns))
+    nc.scalar.copy(out=dst, in_=src)
+    dst, src = views(slice(scalar_columns, raw.shape[2]))
+    nc.vector.tensor_copy(out=dst, in_=src)
+
+
+def tile_picked_deform_lin_none_def_e_kernel(tc, xT, w, offs, out):
+    nc = tc.nc
+    with tc.tile_pool(name="keep", bufs=1) as keep, tc.psum_pool(name="psum", bufs=1) as psum:
+        offsets = keep.tile([P, S // 16], U16, name="offsets")
+
+        warm = keep.tile([P, 1], F32, name="warm")
+        warm_out = keep.tile([P, 1], F32, name="warm_out")
+        nc.vector.memset(warm[:], 0.0)
+        nc.scalar.copy(out=warm_out[:], in_=warm[:])
+
+        x_raw, x_grouped, x_codes, x_scales, g_codes, g_scales = [], [], [], [], [], []
+        for a in range(PASSES):
+            x_raw.append(keep.tile([P, PACK, T], F32, name=f"x_raw{a}"))
+            x_grouped.append(keep.tile([P, T, PACK], BF16, name=f"x_grouped{a}", align_bytes=ALIGN))
+            x_codes.append(keep.tile([P, T], U32, name=f"x_codes{a}", align_bytes=ALIGN))
+            x_scales.append(keep.tile([P, T], U8, name=f"x_scales{a}", align_bytes=ALIGN))
+            g_codes.append(keep.tile([P, S], U32, name=f"g_codes{a}", align_bytes=ALIGN))
+            g_scales.append(keep.tile([P, S], U8, name=f"g_scales{a}", align_bytes=ALIGN))
+            nc.gpsimd.memset(x_scales[a][:], 0)
+
+        blocks = []
+
+        def add_w(d, a, c0, raw):
+            width = raw.shape[2]
+            tag = f"{d}_{a}_{c0}"
+            grouped = keep.tile([P, width, PACK], BF16, name=f"w_grouped{tag}", align_bytes=ALIGN)
+            codes = keep.tile([P, width], U32, name=f"w_codes{tag}", align_bytes=ALIGN)
+            scales = keep.tile([P, width], U8, name=f"w_scales{tag}", align_bytes=ALIGN)
+            blocks.append(("w", d, a, c0, raw, grouped, codes, scales))
+
+        for i, item in enumerate(LOADS):
+            if item[0] == "x":
+                a = item[1]
+                nc.sync.dma_start(out=x_raw[a][:], in_=xT[a * K_PASS : (a + 1) * K_PASS, :].rearrange("(p j) t -> p j t", j=PACK))
+                for c0 in range(0, T, X_HALF):
+                    blocks.append(("x", a, c0))
+            elif len(item) == 2:
+                d = item[1]
+                raw = keep.tile([P, PASSES, PACK, M], F32, name=f"w_raw{d}")
+                nc.sync.dma_start(out=raw[:], in_=w[d].rearrange("(a p j) m -> p a j m", a=PASSES, j=PACK))
+                for a in range(PASSES):
+                    add_w(d, a, 0, raw[:, a, :, :])
+            else:
+                d, a, c0, width = item[1:]
+                rows = w[d, a * K_PASS : (a + 1) * K_PASS, :].rearrange("(p j) m -> p j m", j=PACK)
+                raw = keep.tile([P, PACK, width], F32, name=f"w_raw{d}_{a}_{c0}")
+                nc.sync.dma_start(out=raw[:], in_=rows[:, :, c0 : c0 + width])
+                add_w(d, a, c0, raw[:])
+            if i == 0:
+                nc.sync.dma_start(offsets[:], offs)
+
+        acc = [psum.tile([M_TILE, V], F32, name=f"acc{m}") for m in range(M // M_TILE)]
+        done = [0] * len(acc)
+        gathered = [False] * PASSES
+        waiting = []
+
+        def copy(block):
+            if block[0] == "x":
+                a, c0 = block[1], block[2]
+                cols = slice(c0, c0 + X_HALF)
+                interleave(nc, x_grouped[a][:, cols, :], x_raw[a][:, :, cols], X_SCALAR)
+            else:
+                raw, grouped = block[4], block[5]
+                interleave(nc, grouped[:], raw, w_scalar(raw.shape[2]))
+
+        def multiply(block):
+            d, a, c0, raw, grouped, codes, scales = block[1:]
+            for lo in range(0, raw.shape[2], M_TILE):
+                m = (c0 + lo) // M_TILE
+                nc.tensor.matmul_mx(
+                    out=acc[m][:],
+                    lhsT=codes[:, lo : lo + M_TILE].bitcast(FP8X4),
+                    lhsT_scale=scales[:, lo : lo + M_TILE],
+                    rhs=g_codes[a][:, d * V : (d + 1) * V].bitcast(FP8X4),
+                    rhs_scale=g_scales[a][:, d * V : (d + 1) * V],
+                    start=(done[m] == 0),
+                    stop=(done[m] == D * PASSES - 1),
+                )
+                done[m] += 1
+                if done[m] == D * PASSES:
+                    result = keep.tile([M_TILE, V], F32, name=f"result{m}")
+                    nc.scalar.copy(out=result[:], in_=acc[m][:])
+                    nc.sync.dma_start(out=out[m * M_TILE : (m + 1) * M_TILE, :], in_=result[:])
+
+        def quantize(block):
+            if block[0] == "x":
+                a, c0 = block[1], block[2]
+                cols = slice(c0, c0 + X_HALF)
+                nc.vector.quantize_mx(
+                    out=x_codes[a][:, cols].bitcast(FP8X4),
+                    scales=x_scales[a][:, cols],
+                    in_=x_grouped[a][:, cols, :].rearrange("p c j -> p (c j)"),
+                )
+                if c0 + X_HALF == T:
+                    nc.vector.tensor_copy(g_codes[a][:], x_codes[a][:].indirect(offsets[:]))
+                    nc.vector.tensor_copy(g_scales[a][:], x_scales[a][:].indirect(offsets[:]))
+                    gathered[a] = True
+            else:
+                nc.vector.quantize_mx(
+                    out=block[6][:].bitcast(FP8X4),
+                    scales=block[7][:],
+                    in_=block[5][:].rearrange("p c j -> p (c j)"),
+                )
+                waiting.append(block)
+            for ready in [b for b in waiting if gathered[b[2]]]:
+                waiting.remove(ready)
+                multiply(ready)
+
+        for step in range(len(blocks) + 1):
+            if step < len(blocks):
+                copy(blocks[step])
+            if step > 0:
+                quantize(blocks[step - 1])

@@ -17,27 +17,11 @@ PASSES = K // K_PASS
 M_TILE = 128
 ALIGN = 64
 
-LOADS = (
-    ("x", 0), ("w", 0), ("x", 1), ("w", 1), ("w", 2), ("w", 3, 0, 0, M), ("w", 3, 1, 0, 256), ("w", 3, 1, 256, 128), ("w", 3, 1, 384, 128),
-)
-X_HALF = T // 2
-X_SCALAR = 320
 
-
-def w_scalar(width):
-    return 288 * width // M if width == M else 96 * width // 256
-
-
-def interleave(nc, grouped, raw, scalar_columns):
-    def views(cols):
-        dst = grouped[:, cols, :].rearrange("p (c i) j -> p c j i", i=2)
-        src = raw[:, :, cols].rearrange("p j (c i) -> p c j i", i=2)
-        return dst, src
-
-    dst, src = views(slice(0, scalar_columns))
-    nc.scalar.copy(out=dst, in_=src)
-    dst, src = views(slice(scalar_columns, raw.shape[2]))
-    nc.vector.tensor_copy(out=dst, in_=src)
+def interleave(engine_copy, grouped, raw):
+    dst = grouped.rearrange("p (c i) j -> p c j i", i=2)
+    src = raw.rearrange("p j (c i) -> p c j i", i=2)
+    engine_copy(out=dst, in_=src)
 
 
 def tile_picked_deform_lin_none_def_e_kernel(tc, xT, w, offs, out):
@@ -50,64 +34,71 @@ def tile_picked_deform_lin_none_def_e_kernel(tc, xT, w, offs, out):
         nc.vector.memset(warm[:], 0.0)
         nc.scalar.copy(out=warm_out[:], in_=warm[:])
 
-        x_raw, x_grouped, x_codes, x_scales, g_codes, g_scales = [], [], [], [], [], []
+        x_codes, g_codes, x_scales, g_scales = [], [], [], []
         for a in range(PASSES):
-            x_raw.append(keep.tile([P, PACK, T], F32, name=f"x_raw{a}"))
-            x_grouped.append(keep.tile([P, T, PACK], BF16, name=f"x_grouped{a}", align_bytes=ALIGN))
-            x_codes.append(keep.tile([P, T], U32, name=f"x_codes{a}", align_bytes=ALIGN))
             x_scales.append(keep.tile([P, T], U8, name=f"x_scales{a}", align_bytes=ALIGN))
-            g_codes.append(keep.tile([P, S], U32, name=f"g_codes{a}", align_bytes=ALIGN))
             g_scales.append(keep.tile([P, S], U8, name=f"g_scales{a}", align_bytes=ALIGN))
             nc.gpsimd.memset(x_scales[a][:], 0)
+            x_codes.append(keep.tile([P, T], U32, name=f"x_codes{a}", align_bytes=ALIGN))
+            g_codes.append(keep.tile([P, S], U32, name=f"g_codes{a}", align_bytes=ALIGN))
 
-        blocks = []
+        def load_x(a, c0=0, width=T):
+            raw = keep.tile([P, PACK, width], F32, name=f"x_raw{a}_{c0}")
+            nc.sync.dma_start(out=raw[:], in_=xT[a * K_PASS : (a + 1) * K_PASS, :].rearrange("(p j) t -> p j t", j=PACK)[:, :, c0 : c0 + width])
+            return raw
 
-        def add_w(d, a, c0, raw):
-            width = raw.shape[2]
-            tag = f"{d}_{a}_{c0}"
-            grouped = keep.tile([P, width, PACK], BF16, name=f"w_grouped{tag}", align_bytes=ALIGN)
-            codes = keep.tile([P, width], U32, name=f"w_codes{tag}", align_bytes=ALIGN)
-            scales = keep.tile([P, width], U8, name=f"w_scales{tag}", align_bytes=ALIGN)
-            blocks.append(("w", d, a, c0, raw, grouped, codes, scales))
+        w_passes = w.rearrange("d (a p j) m -> p (d a) j m", a=PASSES, j=PACK)
 
-        for i, item in enumerate(LOADS):
-            if item[0] == "x":
-                a = item[1]
-                nc.sync.dma_start(out=x_raw[a][:], in_=xT[a * K_PASS : (a + 1) * K_PASS, :].rearrange("(p j) t -> p j t", j=PACK))
-                for c0 in range(0, T, X_HALF):
-                    blocks.append(("x", a, c0))
-            elif len(item) == 2:
-                d = item[1]
-                raw = keep.tile([P, PASSES, PACK, M], F32, name=f"w_raw{d}")
-                nc.sync.dma_start(out=raw[:], in_=w[d].rearrange("(a p j) m -> p a j m", a=PASSES, j=PACK))
-                for a in range(PASSES):
-                    add_w(d, a, 0, raw[:, a, :, :])
-            else:
-                d, a, c0, width = item[1:]
-                rows = w[d, a * K_PASS : (a + 1) * K_PASS, :].rearrange("(p j) m -> p j m", j=PACK)
-                raw = keep.tile([P, PACK, width], F32, name=f"w_raw{d}_{a}_{c0}")
-                nc.sync.dma_start(out=raw[:], in_=rows[:, :, c0 : c0 + width])
-                add_w(d, a, c0, raw[:])
-            if i == 0:
-                nc.sync.dma_start(offsets[:], offs)
+        def load_passes(g0, count):
+            raw = keep.tile([P, count, PACK, M], F32, name=f"w_raw{g0}")
+            nc.sync.dma_start(out=raw[:], in_=w_passes[:, g0 : g0 + count, :, :])
+            return raw
+
+        def load_cols(g, c0, width):
+            raw = keep.tile([P, PACK, width], F32, name=f"w_raw{g}_{c0}")
+            nc.sync.dma_start(out=raw[:], in_=w_passes[:, g, :, c0 : c0 + width])
+            return raw
 
         acc = [psum.tile([M_TILE, V], F32, name=f"acc{m}") for m in range(M // M_TILE)]
         done = [0] * len(acc)
-        gathered = [False] * PASSES
-        waiting = []
 
-        def copy(block):
-            if block[0] == "x":
-                a, c0 = block[1], block[2]
-                cols = slice(c0, c0 + X_HALF)
-                interleave(nc, x_grouped[a][:, cols, :], x_raw[a][:, :, cols], X_SCALAR)
-            else:
-                raw, grouped = block[4], block[5]
-                interleave(nc, grouped[:], raw, w_scalar(raw.shape[2]))
+        def copy(name, raw, scalar_columns):
+            width = raw.shape[2]
+            grouped = keep.tile([P, width, PACK], BF16, name=f"grouped_{name}", align_bytes=ALIGN)
+            if scalar_columns > 0:
+                interleave(nc.scalar.copy, grouped[:, 0:scalar_columns, :], raw[:, :, 0:scalar_columns])
+            if scalar_columns < width:
+                interleave(nc.vector.tensor_copy, grouped[:, scalar_columns:, :], raw[:, :, scalar_columns:])
+            return grouped
 
-        def multiply(block):
-            d, a, c0, raw, grouped, codes, scales = block[1:]
-            for lo in range(0, raw.shape[2], M_TILE):
+        def quantize_x(a, c0, grouped):
+            cols = slice(c0, c0 + grouped.shape[1])
+            nc.vector.quantize_mx(
+                out=x_codes[a][:, cols].bitcast(FP8X4),
+                scales=x_scales[a][:, cols],
+                in_=grouped[:].rearrange("p c j -> p (c j)"),
+            )
+
+        def gather_codes(a):
+            nc.vector.tensor_copy(g_codes[a][:], x_codes[a][:].indirect(offsets[:]))
+
+        def gather_scales(a):
+            nc.vector.tensor_copy(g_scales[a][:], x_scales[a][:].indirect(offsets[:]))
+
+        def w_copy(g, c0, raw, scalar_columns):
+            width = raw.shape[2]
+            grouped = copy(f"w{g}_{c0}", raw, scalar_columns)
+            codes = keep.tile([P, width], U32, name=f"w_codes{g}_{c0}", align_bytes=ALIGN)
+            scales = keep.tile([P, width], U8, name=f"w_scales{g}_{c0}", align_bytes=ALIGN)
+            return (g, c0, width, grouped, codes, scales)
+
+        def quantize(pc):
+            nc.vector.quantize_mx(out=pc[4][:].bitcast(FP8X4), scales=pc[5][:], in_=pc[3][:].rearrange("p c j -> p (c j)"))
+
+        def multiply(pc):
+            g, c0, width, grouped, codes, scales = pc
+            d, a = divmod(g, PASSES)
+            for lo in range(0, width, M_TILE):
                 m = (c0 + lo) // M_TILE
                 nc.tensor.matmul_mx(
                     out=acc[m][:],
@@ -119,37 +110,64 @@ def tile_picked_deform_lin_none_def_e_kernel(tc, xT, w, offs, out):
                     stop=(done[m] == D * PASSES - 1),
                 )
                 done[m] += 1
-                if done[m] == D * PASSES:
-                    result = keep.tile([M_TILE, V], F32, name=f"result{m}")
-                    nc.scalar.copy(out=result[:], in_=acc[m][:])
-                    nc.sync.dma_start(out=out[m * M_TILE : (m + 1) * M_TILE, :], in_=result[:])
 
-        def quantize(block):
-            if block[0] == "x":
-                a, c0 = block[1], block[2]
-                cols = slice(c0, c0 + X_HALF)
-                nc.vector.quantize_mx(
-                    out=x_codes[a][:, cols].bitcast(FP8X4),
-                    scales=x_scales[a][:, cols],
-                    in_=x_grouped[a][:, cols, :].rearrange("p c j -> p (c j)"),
-                )
-                if c0 + X_HALF == T:
-                    nc.vector.tensor_copy(g_codes[a][:], x_codes[a][:].indirect(offsets[:]))
-                    nc.vector.tensor_copy(g_scales[a][:], x_scales[a][:].indirect(offsets[:]))
-                    gathered[a] = True
-            else:
-                nc.vector.quantize_mx(
-                    out=block[6][:].bitcast(FP8X4),
-                    scales=block[7][:],
-                    in_=block[5][:].rearrange("p c j -> p (c j)"),
-                )
-                waiting.append(block)
-            for ready in [b for b in waiting if gathered[b[2]]]:
-                waiting.remove(ready)
-                multiply(ready)
+        def finish(pc):
+            quantize(pc)
+            multiply(pc)
 
-        for step in range(len(blocks) + 1):
-            if step < len(blocks):
-                copy(blocks[step])
-            if step > 0:
-                quantize(blocks[step - 1])
+        def store(m0, count, result, copies, queue):
+            for m in range(count):
+                copies[m](out=result[:, m, :], in_=acc[m0 + m][:])
+            queue.dma_start(out=out[m0 * M_TILE : (m0 + count) * M_TILE, :].rearrange("(m p) v -> p m v", p=M_TILE), in_=result)
+
+        sc, vc = nc.scalar.copy, nc.vector.tensor_copy
+
+        x0 = load_x(0)
+        nc.sync.dma_start(offsets[:], offs)
+        x1 = load_x(1)
+        w012 = load_passes(0, 3)
+        w34 = load_passes(3, 2)
+        w5 = load_passes(5, 1)
+        w6 = load_passes(6, 1)
+        wa = load_cols(7, 0, 256)
+        wb = load_cols(7, 256, 128)
+        wc = load_cols(7, 384, 128)
+
+        for a, raw in enumerate((x0, x1)):
+            parts = [(c0, copy(f"x{a}_{c0}", raw[:, :, c0 : c0 + 512], 320)) for c0 in range(0, T, 512)]
+            for c0, grouped in parts:
+                quantize_x(a, c0, grouped)
+            gather_codes(a)
+            gather_scales(a)
+
+
+        def leave(m):
+            result = keep.tile([M_TILE, 1, V], F32, name=f"result{m}")
+            store(m, 1, result[:], (sc,), nc.sync)
+
+
+        held = []
+
+
+        def finish_or_hold(pc):
+            quantize(pc)
+            if pc[0] in (3, 4):
+                held.append(pc)
+                return
+            multiply(pc)
+            if pc[0] == 5:
+                for late in held:
+                    multiply(late)
+            if pc[0] == 7:
+                for m in range(pc[1] // M_TILE, (pc[1] + pc[2]) // M_TILE):
+                    leave(m)
+
+
+        prev = None
+        for g, c0, raw, share in ((0, 0, w012[:, 0], 288), (1, 0, w012[:, 1], 288), (2, 0, w012[:, 2], 288), (3, 0, w34[:, 0], 288), (4, 0, w34[:, 1], 288),
+                                  (5, 0, w5[:, 0], 288), (6, 0, w6[:, 0], 288), (7, 0, wa[:], 96), (7, 256, wb[:], 48), (7, 384, wc[:], 48)):
+            pc = w_copy(g, c0, raw, share)
+            if prev is not None:
+                finish_or_hold(prev)
+            prev = pc
+        finish_or_hold(prev)

@@ -28,23 +28,18 @@ def tile_picked_deform_lin_none_def_e_kernel(tc, xT, w, offs, out):
     nc = tc.nc
     with tc.tile_pool(name="keep", bufs=1) as keep, tc.psum_pool(name="psum", bufs=1) as psum:
         offsets = keep.tile([P, S // 16], U16, name="offsets")
+        sc, vc = nc.scalar.copy, nc.vector.tensor_copy
 
-        warm = keep.tile([P, 1], F32, name="warm")
-        warm_out = keep.tile([P, 1], F32, name="warm_out")
-        nc.vector.memset(warm[:], 0.0)
-        nc.scalar.copy(out=warm_out[:], in_=warm[:])
+        x_scales = [keep.tile([P, T], U8, name=f"x_scales{a}", align_bytes=ALIGN) for a in range(PASSES)]
+        g_scales = [keep.tile([P, S], U8, name=f"g_scales{a}", align_bytes=ALIGN) for a in range(PASSES)]
+        for plane in x_scales:
+            nc.gpsimd.memset(plane[:], 0)
+        x_codes = [keep.tile([P, T], U32, name=f"x_codes{a}", align_bytes=ALIGN) for a in range(PASSES)]
+        g_codes = [keep.tile([P, S], U32, name=f"g_codes{a}", align_bytes=ALIGN) for a in range(PASSES)]
 
-        x_codes, g_codes, x_scales, g_scales = [], [], [], []
-        for a in range(PASSES):
-            x_scales.append(keep.tile([P, T], U8, name=f"x_scales{a}", align_bytes=ALIGN))
-            g_scales.append(keep.tile([P, S], U8, name=f"g_scales{a}", align_bytes=ALIGN))
-            nc.gpsimd.memset(x_scales[a][:], 0)
-            x_codes.append(keep.tile([P, T], U32, name=f"x_codes{a}", align_bytes=ALIGN))
-            g_codes.append(keep.tile([P, S], U32, name=f"g_codes{a}", align_bytes=ALIGN))
-
-        def load_x(a, c0=0, width=T):
-            raw = keep.tile([P, PACK, width], F32, name=f"x_raw{a}_{c0}")
-            nc.sync.dma_start(out=raw[:], in_=xT[a * K_PASS : (a + 1) * K_PASS, :].rearrange("(p j) t -> p j t", j=PACK)[:, :, c0 : c0 + width])
+        def load_x(a):
+            raw = keep.tile([P, PACK, T], F32, name=f"x_raw{a}")
+            nc.sync.dma_start(out=raw[:], in_=xT[a * K_PASS : (a + 1) * K_PASS, :].rearrange("(p j) t -> p j t", j=PACK))
             return raw
 
         w_passes = w.rearrange("d (a p j) m -> p (d a) j m", a=PASSES, j=PACK)
@@ -52,23 +47,25 @@ def tile_picked_deform_lin_none_def_e_kernel(tc, xT, w, offs, out):
         def load_passes(g0, count):
             raw = keep.tile([P, count, PACK, M], F32, name=f"w_raw{g0}")
             nc.sync.dma_start(out=raw[:], in_=w_passes[:, g0 : g0 + count, :, :])
-            return raw
+            return [raw[:, i] for i in range(count)]
 
         def load_cols(g, c0, width):
             raw = keep.tile([P, PACK, width], F32, name=f"w_raw{g}_{c0}")
             nc.sync.dma_start(out=raw[:], in_=w_passes[:, g, :, c0 : c0 + width])
-            return raw
+            return raw[:]
 
         acc = [psum.tile([M_TILE, V], F32, name=f"acc{m}") for m in range(M // M_TILE)]
         done = [0] * len(acc)
 
-        def copy(name, raw, scalar_columns):
+        def copy(name, raw, scalar_columns, grouped=None):
             width = raw.shape[2]
-            grouped = keep.tile([P, width, PACK], BF16, name=f"grouped_{name}", align_bytes=ALIGN)
+            if grouped is None:
+                grouped = keep.tile([P, width, PACK], BF16, name=f"grouped_{name}", align_bytes=ALIGN)[:]
+            cut = width - scalar_columns
             if scalar_columns > 0:
-                interleave(nc.scalar.copy, grouped[:, 0:scalar_columns, :], raw[:, :, 0:scalar_columns])
-            if scalar_columns < width:
-                interleave(nc.vector.tensor_copy, grouped[:, scalar_columns:, :], raw[:, :, scalar_columns:])
+                interleave(sc, grouped[:, cut:, :], raw[:, :, cut:])
+            if cut > 0:
+                interleave(vc, grouped[:, 0:cut, :], raw[:, :, 0:cut])
             return grouped
 
         def quantize_x(a, c0, grouped):
@@ -76,24 +73,18 @@ def tile_picked_deform_lin_none_def_e_kernel(tc, xT, w, offs, out):
             nc.vector.quantize_mx(
                 out=x_codes[a][:, cols].bitcast(FP8X4),
                 scales=x_scales[a][:, cols],
-                in_=grouped[:].rearrange("p c j -> p (c j)"),
+                in_=grouped.rearrange("p c j -> p (c j)"),
             )
 
-        def gather_codes(a):
-            nc.vector.tensor_copy(g_codes[a][:], x_codes[a][:].indirect(offsets[:]))
-
-        def gather_scales(a):
-            nc.vector.tensor_copy(g_scales[a][:], x_scales[a][:].indirect(offsets[:]))
-
-        def w_copy(g, c0, raw, scalar_columns):
+        def w_copy(g, c0, raw, scalar_columns, grouped=None):
             width = raw.shape[2]
-            grouped = copy(f"w{g}_{c0}", raw, scalar_columns)
+            grouped = copy(f"w{g}_{c0}", raw, scalar_columns, grouped)
             codes = keep.tile([P, width], U32, name=f"w_codes{g}_{c0}", align_bytes=ALIGN)
             scales = keep.tile([P, width], U8, name=f"w_scales{g}_{c0}", align_bytes=ALIGN)
             return (g, c0, width, grouped, codes, scales)
 
         def quantize(pc):
-            nc.vector.quantize_mx(out=pc[4][:].bitcast(FP8X4), scales=pc[5][:], in_=pc[3][:].rearrange("p c j -> p (c j)"))
+            nc.vector.quantize_mx(out=pc[4][:].bitcast(FP8X4), scales=pc[5][:], in_=pc[3].rearrange("p c j -> p (c j)"))
 
         def multiply(pc):
             g, c0, width, grouped, codes, scales = pc
@@ -111,63 +102,56 @@ def tile_picked_deform_lin_none_def_e_kernel(tc, xT, w, offs, out):
                 )
                 done[m] += 1
 
+        def leave(m0, copies, queue=nc.sync):
+            result = keep.tile([M_TILE, len(copies), V], F32, name=f"result{m0}")
+            for i, engine_copy in enumerate(copies):
+                engine_copy(out=result[:, i, :], in_=acc[m0 + i][:])
+            queue.dma_start(out=out[m0 * M_TILE : (m0 + len(copies)) * M_TILE, :].rearrange("(m p) v -> p m v", p=M_TILE), in_=result[:])
+
         def finish(pc):
             quantize(pc)
             multiply(pc)
+            for m in range(pc[1] // M_TILE, (pc[1] + pc[2]) // M_TILE):
+                leave(m, (sc,))
 
-        def store(m0, count, result, copies, queue):
-            for m in range(count):
-                copies[m](out=result[:, m, :], in_=acc[m0 + m][:])
-            queue.dma_start(out=out[m0 * M_TILE : (m0 + count) * M_TILE, :].rearrange("(m p) v -> p m v", p=M_TILE), in_=result)
-
-        sc, vc = nc.scalar.copy, nc.vector.tensor_copy
+        def x_work(raws, share):
+            for a, raw in enumerate(raws):
+                parts = [(c0, copy(f"x{a}_{c0}", raw[:, :, c0 : c0 + 512], share)) for c0 in range(0, T, 512)]
+                for c0, grouped in parts:
+                    quantize_x(a, c0, grouped)
+                vc(g_codes[a][:], x_codes[a][:].indirect(offsets[:]))
+                vc(g_scales[a][:], x_scales[a][:].indirect(offsets[:]))
 
         x0 = load_x(0)
         nc.sync.dma_start(offsets[:], offs)
         x1 = load_x(1)
-        w012 = load_passes(0, 3)
-        w34 = load_passes(3, 2)
-        w5 = load_passes(5, 1)
-        w6 = load_passes(6, 1)
-        wa = load_cols(7, 0, 256)
-        wb = load_cols(7, 256, 128)
-        wc = load_cols(7, 384, 128)
+        raws = load_passes(0, 2) + load_passes(2, 2) + load_passes(4, 1) + load_passes(5, 1) + load_passes(6, 1)
+        end_a, end_b, end_c = load_cols(7, 0, 256), load_cols(7, 256, 128), load_cols(7, 384, 128)
 
-        for a, raw in enumerate((x0, x1)):
-            parts = [(c0, copy(f"x{a}_{c0}", raw[:, :, c0 : c0 + 512], 320)) for c0 in range(0, T, 512)]
-            for c0, grouped in parts:
-                quantize_x(a, c0, grouped)
-            gather_codes(a)
-            gather_scales(a)
+        x_work((x0, x1), 352)
 
+        early = {}
+        for group in ((0, 1), (2, 3), (4,), (5,)):
+            for g in group:
+                early[g] = w_copy(g, 0, raws[g], 288 if g < 4 else 208)
+            for g in group:
+                quantize(early[g])
+                if g < 3:
+                    multiply(early[g])
+        for h in (5, 3, 4):
+            multiply(early[h])
 
-        def leave(m):
-            result = keep.tile([M_TILE, 1, V], F32, name=f"result{m}")
-            store(m, 1, result[:], (sc,), nc.sync)
-
-
-        held = []
-
-
-        def finish_or_hold(pc):
-            quantize(pc)
-            if pc[0] in (3, 4):
-                held.append(pc)
-                return
-            multiply(pc)
-            if pc[0] == 5:
-                for late in held:
-                    multiply(late)
-            if pc[0] == 7:
-                for m in range(pc[1] // M_TILE, (pc[1] + pc[2]) // M_TILE):
-                    leave(m)
-
-
-        prev = None
-        for g, c0, raw, share in ((0, 0, w012[:, 0], 288), (1, 0, w012[:, 1], 288), (2, 0, w012[:, 2], 288), (3, 0, w34[:, 0], 288), (4, 0, w34[:, 1], 288),
-                                  (5, 0, w5[:, 0], 288), (6, 0, w6[:, 0], 288), (7, 0, wa[:], 96), (7, 256, wb[:], 48), (7, 384, wc[:], 48)):
-            pc = w_copy(g, c0, raw, share)
-            if prev is not None:
-                finish_or_hold(prev)
-            prev = pc
-        finish_or_hold(prev)
+        six_v = w_copy(6, 0, raws[6][:, :, 0:256], 0)
+        six_s = w_copy(6, 256, raws[6][:, :, 256:512], 256)
+        quantize(six_v)
+        multiply(six_v)
+        a_v = w_copy(7, 0, end_a[:, :, 0:128], 0)
+        a_s = w_copy(7, 128, end_a[:, :, 128:256], 128)
+        quantize(six_s)
+        multiply(six_s)
+        piece_b = w_copy(7, 256, end_b, 128)
+        finish(a_v)
+        finish(a_s)
+        piece_c = w_copy(7, 384, end_c, 0)
+        finish(piece_b)
+        finish(piece_c)

@@ -38,19 +38,19 @@ def tile_picked_deform_lin_none_def_e_kernel(tc, xT, w, offs, out):
         g_codes = [keep.tile([P, S], U32, name=f"g_codes{a}", align_bytes=ALIGN) for a in range(PASSES)]
 
         def load_x(a):
-            raw = keep.tile([P, PACK, T], F32, name=f"x_raw{a}")
+            raw = keep.tile([P, PACK, T], F32, name=f"x_raw{a}", align_bytes=256)
             nc.sync.dma_start(out=raw[:], in_=xT[a * K_PASS : (a + 1) * K_PASS, :].rearrange("(p j) t -> p j t", j=PACK))
             return raw
 
         w_passes = w.rearrange("d (a p j) m -> p (d a) j m", a=PASSES, j=PACK)
 
         def load_passes(g0, count):
-            raw = keep.tile([P, count, PACK, M], F32, name=f"w_raw{g0}")
+            raw = keep.tile([P, count, PACK, M], F32, name=f"w_raw{g0}", align_bytes=256)
             nc.sync.dma_start(out=raw[:], in_=w_passes[:, g0 : g0 + count, :, :])
             return [raw[:, i] for i in range(count)]
 
         def load_cols(g, c0, width):
-            raw = keep.tile([P, PACK, width], F32, name=f"w_raw{g}_{c0}")
+            raw = keep.tile([P, PACK, width], F32, name=f"w_raw{g}_{c0}", align_bytes=256)
             nc.sync.dma_start(out=raw[:], in_=w_passes[:, g, :, c0 : c0 + width])
             return raw[:]
 
@@ -103,7 +103,7 @@ def tile_picked_deform_lin_none_def_e_kernel(tc, xT, w, offs, out):
                 done[m] += 1
 
         def leave(m0, copies, queue=nc.sync):
-            result = keep.tile([M_TILE, len(copies), V], F32, name=f"result{m0}")
+            result = keep.tile([M_TILE, len(copies), V], F32, name=f"result{m0}", align_bytes=256)
             for i, engine_copy in enumerate(copies):
                 engine_copy(out=result[:, i, :], in_=acc[m0 + i][:])
             queue.dma_start(out=out[m0 * M_TILE : (m0 + len(copies)) * M_TILE, :].rearrange("(m p) v -> p m v", p=M_TILE), in_=result[:])

@@ -27,7 +27,7 @@ def interleave(engine_copy, grouped, raw):
 def tile_picked_deform_lin_none_def_e_kernel(tc, xT, w, offs, out):
     nc = tc.nc
     with tc.tile_pool(name="keep", bufs=1) as keep, tc.psum_pool(name="psum", bufs=1) as psum:
-        offsets = keep.tile([P, S // 16], U16, name="offsets")
+        offsets = keep.tile([P, S // 16], U16, name="offsets", align_bytes=256)
         sc, vc = nc.scalar.copy, nc.vector.tensor_copy
 
         x_scales = [keep.tile([P, T], U8, name=f"x_scales{a}", align_bytes=ALIGN) for a in range(PASSES)]
@@ -81,10 +81,14 @@ def tile_picked_deform_lin_none_def_e_kernel(tc, xT, w, offs, out):
             grouped = copy(f"w{g}_{c0}", raw, scalar_columns, grouped)
             codes = keep.tile([P, width], U32, name=f"w_codes{g}_{c0}", align_bytes=ALIGN)
             scales = keep.tile([P, width], U8, name=f"w_scales{g}_{c0}", align_bytes=ALIGN)
-            return (g, c0, width, grouped, codes, scales)
+            return (g, c0, width, grouped, codes[:], scales[:])
+
+        def part(pc, lo, width):
+            g, c0, full, grouped, codes, scales = pc
+            return (g, c0 + lo, width, grouped[:, lo : lo + width, :], codes[:, lo : lo + width], scales[:, lo : lo + width])
 
         def quantize(pc):
-            nc.vector.quantize_mx(out=pc[4][:].bitcast(FP8X4), scales=pc[5][:], in_=pc[3].rearrange("p c j -> p (c j)"))
+            nc.vector.quantize_mx(out=pc[4].bitcast(FP8X4), scales=pc[5], in_=pc[3].rearrange("p c j -> p (c j)"))
 
         def multiply(pc):
             g, c0, width, grouped, codes, scales = pc
@@ -136,22 +140,30 @@ def tile_picked_deform_lin_none_def_e_kernel(tc, xT, w, offs, out):
                 early[g] = w_copy(g, 0, raws[g], 288 if g < 4 else 208)
             for g in group:
                 quantize(early[g])
-                if g < 3:
-                    multiply(early[g])
-        for h in (5, 3, 4):
+        for h in (4, 0, 1, 5, 2):
             multiply(early[h])
 
         six_v = w_copy(6, 0, raws[6][:, :, 0:256], 0)
         six_s = w_copy(6, 256, raws[6][:, :, 256:512], 256)
         quantize(six_v)
         multiply(six_v)
+        multiply(part(early[3], 0, 256))
         a_v = w_copy(7, 0, end_a[:, :, 0:128], 0)
         a_s = w_copy(7, 128, end_a[:, :, 128:256], 128)
         quantize(six_s)
         multiply(six_s)
+        multiply(part(early[3], 256, 256))
         piece_b = w_copy(7, 256, end_b, 128)
         finish(a_v)
         finish(a_s)
-        piece_c = w_copy(7, 384, end_c, 0)
+        grouped_c = keep.tile([P, M_TILE, PACK], BF16, name="grouped_c", align_bytes=ALIGN)
+        codes_c = keep.tile([P, M_TILE], U32, name="codes_c", align_bytes=ALIGN)
+        scales_c = keep.tile([P, M_TILE], U8, name="scales_c", align_bytes=ALIGN)
+        piece_c = (7, 384, M_TILE, grouped_c[:], codes_c[:], scales_c[:])
+        for lo in (0, 64):
+            interleave(vc, grouped_c[:, lo : lo + 64, :], end_c[:, :, lo : lo + 64])
         finish(piece_b)
-        finish(piece_c)
+        for lo in (0, 64):
+            quantize(part(piece_c, lo, 64))
+        multiply(piece_c)
+        leave(3, (sc,))

@@ -12,158 +12,146 @@ FP8X4 = mybir.dt.float8_e4m3fn_x4
 
 P = 128
 PACK = 4
-K_PASS = P * PACK
-PASSES = K // K_PASS
-M_TILE = 128
+PASSES = K // (P * PACK)
+BLOCK = 128
+CHUNK = 512
 ALIGN = 64
-
-
-def interleave(engine_copy, grouped, raw):
-    dst = grouped.rearrange("p (c i) j -> p c j i", i=2)
-    src = raw.rearrange("p j (c i) -> p c j i", i=2)
-    engine_copy(out=dst, in_=src)
+DMA_ALIGN = 256
 
 
 def tile_picked_deform_lin_none_def_e_kernel(tc, xT, w, offs, out):
     nc = tc.nc
+
+    def views(rounded, raw):
+        return rounded.rearrange("p (c i) j -> p c j i", i=2), raw.rearrange("p j (c i) -> p c j i", i=2)
+
+    def round_vector(rounded, raw):
+        dst, src = views(rounded, raw)
+        nc.vector.tensor_copy(out=dst, in_=src)
+
+    def round_scalar(rounded, raw):
+        dst, src = views(rounded, raw)
+        nc.scalar.copy(out=dst, in_=src)
+
+    def round_gpsimd(rounded, raw):
+        nc.gpsimd.tensor_scalar(out=rounded, in0=raw.rearrange("p j c -> p c j"), scalar1=1.0, scalar2=0.0, op0=mybir.AluOpType.mult, op1=mybir.AluOpType.add)
+
+    def quantize(codes, scales, rounded):
+        nc.vector.quantize_mx(out=codes.bitcast(FP8X4), scales=scales, in_=rounded.rearrange("p c j -> p (c j)"))
+
     with tc.tile_pool(name="keep", bufs=1) as keep, tc.psum_pool(name="psum", bufs=1) as psum:
-        offsets = keep.tile([P, S // 16], U16, name="offsets", align_bytes=256)
-        sc, vc = nc.scalar.copy, nc.vector.tensor_copy
-
-        x_scales = [keep.tile([P, T], U8, name=f"x_scales{a}", align_bytes=ALIGN) for a in range(PASSES)]
-        g_scales = [keep.tile([P, S], U8, name=f"g_scales{a}", align_bytes=ALIGN) for a in range(PASSES)]
-        for plane in x_scales:
-            nc.gpsimd.memset(plane[:], 0)
-        x_codes = [keep.tile([P, T], U32, name=f"x_codes{a}", align_bytes=ALIGN) for a in range(PASSES)]
-        g_codes = [keep.tile([P, S], U32, name=f"g_codes{a}", align_bytes=ALIGN) for a in range(PASSES)]
-
-        def load_x(a):
-            raw = keep.tile([P, PACK, T], F32, name=f"x_raw{a}", align_bytes=256)
-            nc.sync.dma_start(out=raw[:], in_=xT[a * K_PASS : (a + 1) * K_PASS, :].rearrange("(p j) t -> p j t", j=PACK))
-            return raw
+        offsets = keep.tile([P, S // 16], U16, name="offsets", align_bytes=DMA_ALIGN)
+        x_raw = keep.tile([P, PASSES, PACK, T], F32, name="x_raw", align_bytes=DMA_ALIGN)
+        nc.sync.dma_start(out=x_raw[:], in_=xT.rearrange("(a p j) t -> p a j t", a=PASSES, j=PACK))
+        nc.sync.dma_start(offsets[:], offs)
 
         w_passes = w.rearrange("d (a p j) m -> p (d a) j m", a=PASSES, j=PACK)
+        w_raw = []
+        for first, count in ((0, 3), (3, 2), (5, 1), (6, 1)):
+            raw = keep.tile([P, count, PACK, M], F32, name=f"w_raw{first}", align_bytes=DMA_ALIGN)
+            nc.sync.dma_start(out=raw[:], in_=w_passes[:, first : first + count])
+            w_raw.extend(raw[:, i] for i in range(count))
+        half = M // 2
+        low_raw = keep.tile([P, PACK, half], F32, name="low_raw", align_bytes=DMA_ALIGN)
+        nc.sync.dma_start(out=low_raw[:], in_=w_passes[:, 7, :, 0:half])
+        shared = keep.tile([P, 192 + PACK * half], F32, name="high_raw", align_bytes=DMA_ALIGN)
+        high_raw = shared[:, 192:].rearrange("p (j c) -> p j c", j=PACK)
+        nc.sync.dma_start(out=high_raw, in_=w_passes[:, 7, :, half:M])
 
-        def load_passes(g0, count):
-            raw = keep.tile([P, count, PACK, M], F32, name=f"w_raw{g0}", align_bytes=256)
-            nc.sync.dma_start(out=raw[:], in_=w_passes[:, g0 : g0 + count, :, :])
-            return [raw[:, i] for i in range(count)]
+        x_scales = keep.tile([P, T], U8, name="x_scales", align_bytes=ALIGN)
+        nc.gpsimd.memset(x_scales[:], 0)
+        x_codes = [keep.tile([P, T], U32, name=f"x_codes{a}", align_bytes=ALIGN) for a in range(PASSES)]
+        picked_codes = [keep.tile([P, S], U32, name=f"picked_codes{a}", align_bytes=ALIGN) for a in range(PASSES)]
+        picked_scales = keep.tile([P, S], U8, name="picked_scales", align_bytes=ALIGN)
 
-        def load_cols(g, c0, width):
-            raw = keep.tile([P, PACK, width], F32, name=f"w_raw{g}_{c0}", align_bytes=256)
-            nc.sync.dma_start(out=raw[:], in_=w_passes[:, g, :, c0 : c0 + width])
-            return raw[:]
+        vector_share_of_x = (256, 256, 192, 128)
+        for i, cut in enumerate(vector_share_of_x):
+            a, c0 = i // 2, (i % 2) * CHUNK
+            rounded = keep.tile([P, CHUNK, PACK], BF16, name=f"rounded_x{i}", tag=f"rounded_x{i}", bufs=1, align_bytes=ALIGN)
+            round_scalar(rounded[:, cut:, :], x_raw[:, a, :, c0 + cut : c0 + CHUNK])
+            round_vector(rounded[:, 0:cut, :], x_raw[:, a, :, c0 : c0 + cut])
+            quantize(x_codes[a][:, c0 : c0 + CHUNK], x_scales[4 * a : P, c0 : c0 + CHUNK], rounded[:])
+            if i % 2 == 1:
+                nc.vector.tensor_copy(picked_codes[a][:], x_codes[a][:].indirect(offsets[:]))
+        nc.vector.tensor_copy(picked_scales[:], x_scales[:].indirect(offsets[:]))
 
-        acc = [psum.tile([M_TILE, V], F32, name=f"acc{m}") for m in range(M // M_TILE)]
-        done = [0] * len(acc)
+        w_codes = [keep.tile([P, M], U32, name=f"w_codes{g}", align_bytes=ALIGN) for g in range(D * PASSES)]
+        w_scales = [keep.tile([P, M], U8, name=f"w_scales{g}", align_bytes=ALIGN) for g in range(D * PASSES)]
+        w_rounded = [keep.tile([P, M, PACK], BF16, name="rounded_x3", tag="rounded_x3", bufs=1, align_bytes=ALIGN)]
+        w_rounded.extend(keep.tile([P, M, PACK], BF16, name=f"rounded_w{g}", align_bytes=ALIGN) for g in range(1, D * PASSES))
 
-        def copy(name, raw, scalar_columns, grouped=None):
-            width = raw.shape[2]
-            if grouped is None:
-                grouped = keep.tile([P, width, PACK], BF16, name=f"grouped_{name}", align_bytes=ALIGN)[:]
-            cut = width - scalar_columns
-            if scalar_columns > 0:
-                interleave(sc, grouped[:, cut:, :], raw[:, :, cut:])
-            if cut > 0:
-                interleave(vc, grouped[:, 0:cut, :], raw[:, :, 0:cut])
-            return grouped
+        pair = psum.tile([BLOCK, 2, V], F32, name="pair")
+        acc = [pair[:, 0, :], pair[:, 1, :]] + [psum.tile([BLOCK, V], F32, name=f"acc{m}")[:] for m in (2, 3)]
+        bank_of = (0, 0, 1, 2)
+        passes_of_bank = (2 * D * PASSES, D * PASSES, D * PASSES)
+        done = [0, 0, 0]
 
-        def quantize_x(a, c0, grouped):
-            cols = slice(c0, c0 + grouped.shape[1])
-            nc.vector.quantize_mx(
-                out=x_codes[a][:, cols].bitcast(FP8X4),
-                scales=x_scales[a][:, cols],
-                in_=grouped.rearrange("p c j -> p (c j)"),
-            )
+        def quantize_w(g, c0, c1):
+            quantize(w_codes[g][:, c0:c1], w_scales[g][:, c0:c1], w_rounded[g][:, c0:c1, :])
 
-        def w_copy(g, c0, raw, scalar_columns, grouped=None):
-            width = raw.shape[2]
-            grouped = copy(f"w{g}_{c0}", raw, scalar_columns, grouped)
-            codes = keep.tile([P, width], U32, name=f"w_codes{g}_{c0}", align_bytes=ALIGN)
-            scales = keep.tile([P, width], U8, name=f"w_scales{g}_{c0}", align_bytes=ALIGN)
-            return (g, c0, width, grouped, codes[:], scales[:])
-
-        def part(pc, lo, width):
-            g, c0, full, grouped, codes, scales = pc
-            return (g, c0 + lo, width, grouped[:, lo : lo + width, :], codes[:, lo : lo + width], scales[:, lo : lo + width])
-
-        def quantize(pc):
-            nc.vector.quantize_mx(out=pc[4].bitcast(FP8X4), scales=pc[5], in_=pc[3].rearrange("p c j -> p (c j)"))
-
-        def multiply(pc):
-            g, c0, width, grouped, codes, scales = pc
+        def multiply(g, blocks):
             d, a = divmod(g, PASSES)
-            for lo in range(0, width, M_TILE):
-                m = (c0 + lo) // M_TILE
+            for m in blocks:
+                bank = bank_of[m]
                 nc.tensor.matmul_mx(
-                    out=acc[m][:],
-                    lhsT=codes[:, lo : lo + M_TILE].bitcast(FP8X4),
-                    lhsT_scale=scales[:, lo : lo + M_TILE],
-                    rhs=g_codes[a][:, d * V : (d + 1) * V].bitcast(FP8X4),
-                    rhs_scale=g_scales[a][:, d * V : (d + 1) * V],
-                    start=(done[m] == 0),
-                    stop=(done[m] == D * PASSES - 1),
+                    out=acc[m],
+                    lhsT=w_codes[g][:, m * BLOCK : (m + 1) * BLOCK].bitcast(FP8X4),
+                    lhsT_scale=w_scales[g][:, m * BLOCK : (m + 1) * BLOCK],
+                    rhs=picked_codes[a][:, d * V : (d + 1) * V].bitcast(FP8X4),
+                    rhs_scale=picked_scales[4 * a : P, d * V : (d + 1) * V],
+                    start=(done[bank] == 0),
+                    stop=(done[bank] == passes_of_bank[bank] - 1),
                 )
-                done[m] += 1
+                done[bank] += 1
 
-        def leave(m0, copies, queue=nc.sync):
-            result = keep.tile([M_TILE, len(copies), V], F32, name=f"result{m0}", align_bytes=256)
-            for i, engine_copy in enumerate(copies):
-                engine_copy(out=result[:, i, :], in_=acc[m0 + i][:])
-            queue.dma_start(out=out[m0 * M_TILE : (m0 + len(copies)) * M_TILE, :].rearrange("(m p) v -> p m v", p=M_TILE), in_=result[:])
+        def round_shared(g, cut, first_engine=round_vector):
+            round_scalar(w_rounded[g][:, cut:, :], w_raw[g][:, :, cut:])
+            first_engine(w_rounded[g][:, 0:cut, :], w_raw[g][:, :, 0:cut])
 
-        def finish(pc):
-            quantize(pc)
-            multiply(pc)
-            for m in range(pc[1] // M_TILE, (pc[1] + pc[2]) // M_TILE):
-                leave(m, (sc,))
+        round_shared(1, 96)
+        round_shared(0, 384, round_gpsimd)
+        round_shared(2, 192)
+        for g in (1, 2):
+            quantize_w(g, 0, M)
+        for g in (3, 4):
+            round_shared(g, 224)
+        for g in (0, 3, 4):
+            quantize_w(g, 0, M)
+        for g in (3, 0, 4, 1):
+            multiply(g, range(4))
 
-        def x_work(raws, share):
-            for a, raw in enumerate(raws):
-                parts = [(c0, copy(f"x{a}_{c0}", raw[:, :, c0 : c0 + 512], share)) for c0 in range(0, T, 512)]
-                for c0, grouped in parts:
-                    quantize_x(a, c0, grouped)
-                vc(g_codes[a][:], x_codes[a][:].indirect(offsets[:]))
-                vc(g_scales[a][:], x_scales[a][:].indirect(offsets[:]))
+        for g in (5, 6):
+            round_shared(g, half)
+            quantize_w(g, 0, half)
+            multiply(g, (0, 1))
+            if g == 5:
+                quantize_w(g, half, M)
+                multiply(g, (2, 3))
+        multiply(2, (0, 1))
 
-        x0 = load_x(0)
-        nc.sync.dma_start(offsets[:], offs)
-        x1 = load_x(1)
-        raws = load_passes(0, 2) + load_passes(2, 2) + load_passes(4, 1) + load_passes(5, 1) + load_passes(6, 1)
-        end_a, end_b, end_c = load_cols(7, 0, 256), load_cols(7, 256, 128), load_cols(7, 384, 128)
+        last = w_rounded[7]
+        round_vector(last[:, 0:128, :], low_raw[:, :, 0:128])
+        round_scalar(last[:, 128:256, :], low_raw[:, :, 128:256])
+        quantize_w(6, half, M)
+        multiply(6, (2, 3))
+        multiply(2, (2, 3))
+        for m in (0, 1):
+            quantize_w(7, m * BLOCK, (m + 1) * BLOCK)
+            multiply(7, (m,))
+        round_scalar(last[:, 256:352, :], high_raw[:, :, 0:96])
+        for lo in (128, 192):
+            round_vector(last[:, half + lo : half + lo + 64, :], high_raw[:, :, lo : lo + 64])
+        round_vector(last[:, 352:384, :], high_raw[:, :, 96:128])
 
-        x_work((x0, x1), 352)
-
-        early = {}
-        for group in ((0, 1), (2, 3), (4,), (5,)):
-            for g in group:
-                early[g] = w_copy(g, 0, raws[g], 288 if g < 4 else 208)
-            for g in group:
-                quantize(early[g])
-        for h in (4, 0, 1, 5, 2):
-            multiply(early[h])
-
-        six_v = w_copy(6, 0, raws[6][:, :, 0:256], 0)
-        six_s = w_copy(6, 256, raws[6][:, :, 256:512], 256)
-        quantize(six_v)
-        multiply(six_v)
-        multiply(part(early[3], 0, 256))
-        a_v = w_copy(7, 0, end_a[:, :, 0:128], 0)
-        a_s = w_copy(7, 128, end_a[:, :, 128:256], 128)
-        quantize(six_s)
-        multiply(six_s)
-        multiply(part(early[3], 256, 256))
-        piece_b = w_copy(7, 256, end_b, 128)
-        finish(a_v)
-        finish(a_s)
-        grouped_c = keep.tile([P, M_TILE, PACK], BF16, name="grouped_c", align_bytes=ALIGN)
-        codes_c = keep.tile([P, M_TILE], U32, name="codes_c", align_bytes=ALIGN)
-        scales_c = keep.tile([P, M_TILE], U8, name="scales_c", align_bytes=ALIGN)
-        piece_c = (7, 384, M_TILE, grouped_c[:], codes_c[:], scales_c[:])
-        for lo in (0, 64):
-            interleave(vc, grouped_c[:, lo : lo + 64, :], end_c[:, :, lo : lo + 64])
-        finish(piece_b)
-        for lo in (0, 64):
-            quantize(part(piece_c, lo, 64))
-        multiply(piece_c)
-        leave(3, (sc,))
+        first_pair = shared[:, 0 : 2 * V].rearrange("p (m v) -> p m v", m=2)
+        nc.scalar.copy(out=first_pair, in_=pair[:])
+        nc.sync.dma_start(out=out[0 : 2 * BLOCK, :].rearrange("(m p) v -> p m v", p=BLOCK), in_=first_pair)
+        for lo in (384, 448):
+            quantize_w(7, lo, lo + 64)
+        multiply(7, (3,))
+        quantize_w(7, 256, 384)
+        multiply(7, (2,))
+        for m, engine_copy in ((3, nc.scalar.copy), (2, nc.vector.tensor_copy)):
+            result = keep.tile([BLOCK, V], F32, name=f"result{m}", align_bytes=DMA_ALIGN)
+            engine_copy(out=result[:], in_=acc[m])
+            nc.sync.dma_start(out=out[m * BLOCK : (m + 1) * BLOCK, :], in_=result[:])

@@ -33,9 +33,6 @@ def tile_picked_deform_lin_none_def_e_kernel(tc, xT, w, offs, out):
         dst, src = views(rounded, raw)
         nc.scalar.copy(out=dst, in_=src)
 
-    def round_gpsimd(rounded, raw):
-        nc.gpsimd.tensor_scalar(out=rounded, in0=raw.rearrange("p j c -> p c j"), scalar1=1.0, scalar2=0.0, op0=mybir.AluOpType.mult, op1=mybir.AluOpType.add)
-
     def quantize(codes, scales, rounded):
         nc.vector.quantize_mx(out=codes.bitcast(FP8X4), scales=scales, in_=rounded.rearrange("p c j -> p (c j)"))
 
@@ -67,7 +64,7 @@ def tile_picked_deform_lin_none_def_e_kernel(tc, xT, w, offs, out):
         vector_share_of_x = (256, 256, 192, 128)
         for i, cut in enumerate(vector_share_of_x):
             a, c0 = i // 2, (i % 2) * CHUNK
-            rounded = keep.tile([P, CHUNK, PACK], BF16, name=f"rounded_x{i}", tag=f"rounded_x{i}", bufs=1, align_bytes=ALIGN)
+            rounded = keep.tile([P, CHUNK, PACK], BF16, name=f"rounded_x{i}", align_bytes=ALIGN)
             round_scalar(rounded[:, cut:, :], x_raw[:, a, :, c0 + cut : c0 + CHUNK])
             round_vector(rounded[:, 0:cut, :], x_raw[:, a, :, c0 : c0 + cut])
             quantize(x_codes[a][:, c0 : c0 + CHUNK], x_scales[4 * a : P, c0 : c0 + CHUNK], rounded[:])
@@ -77,8 +74,7 @@ def tile_picked_deform_lin_none_def_e_kernel(tc, xT, w, offs, out):
 
         w_codes = [keep.tile([P, M], U32, name=f"w_codes{g}", align_bytes=ALIGN) for g in range(D * PASSES)]
         w_scales = [keep.tile([P, M], U8, name=f"w_scales{g}", align_bytes=ALIGN) for g in range(D * PASSES)]
-        w_rounded = [keep.tile([P, M, PACK], BF16, name="rounded_x3", tag="rounded_x3", bufs=1, align_bytes=ALIGN)]
-        w_rounded.extend(keep.tile([P, M, PACK], BF16, name=f"rounded_w{g}", align_bytes=ALIGN) for g in range(1, D * PASSES))
+        w_rounded = [keep.tile([P, M, PACK], BF16, name=f"rounded_w{g}", align_bytes=ALIGN) for g in range(D * PASSES)]
 
         pair = psum.tile([BLOCK, 2, V], F32, name="pair")
         acc = [pair[:, 0, :], pair[:, 1, :]] + [psum.tile([BLOCK, V], F32, name=f"acc{m}")[:] for m in (2, 3)]
@@ -104,29 +100,35 @@ def tile_picked_deform_lin_none_def_e_kernel(tc, xT, w, offs, out):
                 )
                 done[bank] += 1
 
-        def round_shared(g, cut, first_engine=round_vector):
+        def round_shared(g, cut):
             round_scalar(w_rounded[g][:, cut:, :], w_raw[g][:, :, cut:])
-            first_engine(w_rounded[g][:, 0:cut, :], w_raw[g][:, :, 0:cut])
+            round_vector(w_rounded[g][:, 0:cut, :], w_raw[g][:, :, 0:cut])
 
-        round_shared(1, 96)
-        round_shared(0, 384, round_gpsimd)
-        round_shared(2, 192)
-        for g in (1, 2):
+        round_scalar(w_rounded[0][:], w_raw[0])
+        round_shared(1, 192)
+        round_shared(2, 256)
+        for g in (0, 1, 2):
             quantize_w(g, 0, M)
         for g in (3, 4):
             round_shared(g, 224)
-        for g in (0, 3, 4):
+        for g in (3, 4):
             quantize_w(g, 0, M)
         for g in (3, 0, 4, 1):
             multiply(g, range(4))
 
-        for g in (5, 6):
-            round_shared(g, half)
-            quantize_w(g, 0, half)
-            multiply(g, (0, 1))
-            if g == 5:
-                quantize_w(g, half, M)
-                multiply(g, (2, 3))
+        round_scalar(w_rounded[5][:, 192:half, :], w_raw[5][:, :, 192:half])
+        round_scalar(w_rounded[5][:, half:, :], w_raw[5][:, :, half:])
+        round_vector(w_rounded[5][:, 0:192, :], w_raw[5][:, :, 0:192])
+        quantize_w(5, 0, half)
+        multiply(5, (0, 1))
+        quantize_w(5, half, M)
+        multiply(5, (2, 3))
+        round_scalar(w_rounded[6][:, half:, :], w_raw[6][:, :, half:])
+        for m in (0, 1):
+            round_vector(w_rounded[6][:, m * BLOCK : (m + 1) * BLOCK, :], w_raw[6][:, :, m * BLOCK : (m + 1) * BLOCK])
+        for m in (0, 1):
+            quantize_w(6, m * BLOCK, (m + 1) * BLOCK)
+        multiply(6, (0, 1))
         multiply(2, (0, 1))
 
         last = w_rounded[7]

@@ -61,7 +61,7 @@ def tile_picked_deform_lin_none_def_e_kernel(tc, xT, w, offs, out):
         picked_codes = [keep.tile([P, S], U32, name=f"picked_codes{a}", align_bytes=ALIGN) for a in range(PASSES)]
         picked_scales = keep.tile([P, S], U8, name="picked_scales", align_bytes=ALIGN)
 
-        vector_share_of_x = (256, 256, 192, 128)
+        vector_share_of_x = (256, 256, 256, 192)
         for i, cut in enumerate(vector_share_of_x):
             a, c0 = i // 2, (i % 2) * CHUNK
             rounded = keep.tile([P, CHUNK, PACK], BF16, name=f"rounded_x{i}", align_bytes=ALIGN)
@@ -105,30 +105,27 @@ def tile_picked_deform_lin_none_def_e_kernel(tc, xT, w, offs, out):
             round_vector(w_rounded[g][:, 0:cut, :], w_raw[g][:, :, 0:cut])
 
         round_scalar(w_rounded[0][:], w_raw[0])
-        round_shared(1, 192)
-        round_shared(2, 256)
+        round_shared(1, 3 * BLOCK)
+        round_shared(2, half)
         for g in (0, 1, 2):
             quantize_w(g, 0, M)
         for g in (3, 4):
-            round_shared(g, 224)
+            round_shared(g, half)
         for g in (3, 4):
             quantize_w(g, 0, M)
         for g in (3, 0, 4, 1):
             multiply(g, range(4))
 
-        round_scalar(w_rounded[5][:, 192:half, :], w_raw[5][:, :, 192:half])
-        round_scalar(w_rounded[5][:, half:, :], w_raw[5][:, :, half:])
-        round_vector(w_rounded[5][:, 0:192, :], w_raw[5][:, :, 0:192])
-        quantize_w(5, 0, half)
-        multiply(5, (0, 1))
-        quantize_w(5, half, M)
-        multiply(5, (2, 3))
-        round_scalar(w_rounded[6][:, half:, :], w_raw[6][:, :, half:])
-        for m in (0, 1):
-            round_vector(w_rounded[6][:, m * BLOCK : (m + 1) * BLOCK, :], w_raw[6][:, :, m * BLOCK : (m + 1) * BLOCK])
-        for m in (0, 1):
-            quantize_w(6, m * BLOCK, (m + 1) * BLOCK)
-        multiply(6, (0, 1))
+        for g in (5, 6):
+            round_scalar(w_rounded[g][:, half:, :], w_raw[g][:, :, half:])
+            for m in (0, 1):
+                round_vector(w_rounded[g][:, m * BLOCK : (m + 1) * BLOCK, :], w_raw[g][:, :, m * BLOCK : (m + 1) * BLOCK])
+            for m in (0, 1):
+                quantize_w(g, m * BLOCK, (m + 1) * BLOCK)
+            multiply(g, (0, 1))
+            if g == 5:
+                quantize_w(g, half, M)
+                multiply(g, (2, 3))
         multiply(2, (0, 1))
 
         last = w_rounded[7]
@@ -140,10 +137,10 @@ def tile_picked_deform_lin_none_def_e_kernel(tc, xT, w, offs, out):
         for m in (0, 1):
             quantize_w(7, m * BLOCK, (m + 1) * BLOCK)
             multiply(7, (m,))
-        round_scalar(last[:, 256:352, :], high_raw[:, :, 0:96])
+        round_scalar(last[:, 256:336, :], high_raw[:, :, 0:80])
         for lo in (128, 192):
             round_vector(last[:, half + lo : half + lo + 64, :], high_raw[:, :, lo : lo + 64])
-        round_vector(last[:, 352:384, :], high_raw[:, :, 96:128])
+        round_vector(last[:, 336:384, :], high_raw[:, :, 80:128])
 
         first_pair = shared[:, 0 : 2 * V].rearrange("p (m v) -> p m v", m=2)
         nc.scalar.copy(out=first_pair, in_=pair[:])

@@ -38,9 +38,11 @@ def tile_picked_deform_lin_none_def_e_kernel(tc, xT, w, offs, out):
 
     with tc.tile_pool(name="keep", bufs=1) as keep, tc.psum_pool(name="psum", bufs=1) as psum:
         offsets = keep.tile([P, S // 16], U16, name="offsets", align_bytes=DMA_ALIGN)
-        x_raw = keep.tile([P, PASSES, PACK, T], F32, name="x_raw", align_bytes=DMA_ALIGN)
-        nc.sync.dma_start(out=x_raw[:], in_=xT.rearrange("(a p j) t -> p a j t", a=PASSES, j=PACK))
+        x_passes = xT.rearrange("(a p j) t -> a p j t", a=PASSES, j=PACK)
+        x_raw = [keep.tile([P, PACK, T], F32, name=f"x_raw{a}", align_bytes=DMA_ALIGN) for a in range(PASSES)]
+        nc.sync.dma_start(out=x_raw[0][:], in_=x_passes[0])
         nc.sync.dma_start(offsets[:], offs)
+        nc.sync.dma_start(out=x_raw[1][:], in_=x_passes[1])
 
         w_passes = w.rearrange("d (a p j) m -> p (d a) j m", a=PASSES, j=PACK)
         w_raw = []
@@ -61,12 +63,12 @@ def tile_picked_deform_lin_none_def_e_kernel(tc, xT, w, offs, out):
         picked_codes = [keep.tile([P, S], U32, name=f"picked_codes{a}", align_bytes=ALIGN) for a in range(PASSES)]
         picked_scales = keep.tile([P, S], U8, name="picked_scales", align_bytes=ALIGN)
 
-        vector_share_of_x = (256, 256, 256, 192)
+        vector_share_of_x = (256, 256, 256, 256)
         for i, cut in enumerate(vector_share_of_x):
             a, c0 = i // 2, (i % 2) * CHUNK
             rounded = keep.tile([P, CHUNK, PACK], BF16, name=f"rounded_x{i}", align_bytes=ALIGN)
-            round_scalar(rounded[:, cut:, :], x_raw[:, a, :, c0 + cut : c0 + CHUNK])
-            round_vector(rounded[:, 0:cut, :], x_raw[:, a, :, c0 : c0 + cut])
+            round_scalar(rounded[:, cut:, :], x_raw[a][:, :, c0 + cut : c0 + CHUNK])
+            round_vector(rounded[:, 0:cut, :], x_raw[a][:, :, c0 : c0 + cut])
             quantize(x_codes[a][:, c0 : c0 + CHUNK], x_scales[4 * a : P, c0 : c0 + CHUNK], rounded[:])
             if i % 2 == 1:
                 nc.vector.tensor_copy(picked_codes[a][:], x_codes[a][:].indirect(offsets[:]))
@@ -104,13 +106,12 @@ def tile_picked_deform_lin_none_def_e_kernel(tc, xT, w, offs, out):
             round_scalar(w_rounded[g][:, cut:, :], w_raw[g][:, :, cut:])
             round_vector(w_rounded[g][:, 0:cut, :], w_raw[g][:, :, 0:cut])
 
-        round_scalar(w_rounded[0][:], w_raw[0])
-        round_shared(1, 3 * BLOCK)
-        round_shared(2, half)
+        for g in (0, 1, 2):
+            round_shared(g, half)
         for g in (0, 1, 2):
             quantize_w(g, 0, M)
         for g in (3, 4):
-            round_shared(g, half)
+            round_shared(g, 288)
         for g in (3, 4):
             quantize_w(g, 0, M)
         for g in (3, 0, 4, 1):

@@ -45,11 +45,12 @@ def tile_picked_deform_lin_none_def_e_kernel(tc, xT, w, offs, out):
         nc.sync.dma_start(out=x_raw[1][:], in_=x_passes[1])
 
         w_passes = w.rearrange("d (a p j) m -> p (d a) j m", a=PASSES, j=PACK)
-        w_raw = []
+        w_raw, w_loads = [], []
         for first, count in ((0, 3), (3, 2), (5, 1), (6, 1)):
             raw = keep.tile([P, count, PACK, M], F32, name=f"w_raw{first}", align_bytes=DMA_ALIGN)
             nc.sync.dma_start(out=raw[:], in_=w_passes[:, first : first + count])
             w_raw.extend(raw[:, i] for i in range(count))
+            w_loads.append(raw)
         half = M // 2
         low_raw = keep.tile([P, PACK, half], F32, name="low_raw", align_bytes=DMA_ALIGN)
         nc.sync.dma_start(out=low_raw[:], in_=w_passes[:, 7, :, 0:half])
@@ -63,20 +64,23 @@ def tile_picked_deform_lin_none_def_e_kernel(tc, xT, w, offs, out):
         picked_codes = [keep.tile([P, S], U32, name=f"picked_codes{a}", align_bytes=ALIGN) for a in range(PASSES)]
         picked_scales = keep.tile([P, S], U8, name="picked_scales", align_bytes=ALIGN)
 
-        vector_share_of_x = (256, 256, 256, 256)
-        for i, cut in enumerate(vector_share_of_x):
-            a, c0 = i // 2, (i % 2) * CHUNK
-            rounded = keep.tile([P, CHUNK, PACK], BF16, name=f"rounded_x{i}", align_bytes=ALIGN)
-            round_scalar(rounded[:, cut:, :], x_raw[a][:, :, c0 + cut : c0 + CHUNK])
-            round_vector(rounded[:, 0:cut, :], x_raw[a][:, :, c0 : c0 + cut])
-            quantize(x_codes[a][:, c0 : c0 + CHUNK], x_scales[4 * a : P, c0 : c0 + CHUNK], rounded[:])
-            if i % 2 == 1:
-                nc.vector.tensor_copy(picked_codes[a][:], x_codes[a][:].indirect(offsets[:]))
+        vector_share_of_x = 576
+        for a in range(PASSES):
+            rounded = keep.tile([P, T, PACK], BF16, name=f"rounded_x{a}", align_bytes=ALIGN)
+            round_scalar(rounded[:, vector_share_of_x:, :], x_raw[a][:, :, vector_share_of_x:])
+            round_vector(rounded[:, 0:vector_share_of_x, :], x_raw[a][:, :, 0:vector_share_of_x])
+            width = T if a == 0 else CHUNK
+            for c0 in range(0, T, width):
+                quantize(x_codes[a][:, c0 : c0 + width], x_scales[4 * a : P, c0 : c0 + width], rounded[:, c0 : c0 + width, :])
+            nc.vector.tensor_copy(picked_codes[a][:], x_codes[a][:].indirect(offsets[:]))
         nc.vector.tensor_copy(picked_scales[:], x_scales[:].indirect(offsets[:]))
 
-        w_codes = [keep.tile([P, M], U32, name=f"w_codes{g}", align_bytes=ALIGN) for g in range(D * PASSES)]
-        w_scales = [keep.tile([P, M], U8, name=f"w_scales{g}", align_bytes=ALIGN) for g in range(D * PASSES)]
-        w_rounded = [keep.tile([P, M, PACK], BF16, name=f"rounded_w{g}", align_bytes=ALIGN) for g in range(D * PASSES)]
+        all_codes = keep.tile([P, D * PASSES, M], U32, name="w_codes", align_bytes=ALIGN)
+        all_scales = keep.tile([P, D * PASSES, M], U8, name="w_scales", align_bytes=ALIGN)
+        all_rounded = keep.tile([P, D * PASSES, M, PACK], BF16, name="w_rounded", align_bytes=ALIGN)
+        w_codes = [all_codes[:, g] for g in range(D * PASSES)]
+        w_scales = [all_scales[:, g] for g in range(D * PASSES)]
+        w_rounded = [all_rounded[:, g] for g in range(D * PASSES)]
 
         pair = psum.tile([BLOCK, 2, V], F32, name="pair")
         acc = [pair[:, 0, :], pair[:, 1, :]] + [psum.tile([BLOCK, V], F32, name=f"acc{m}")[:] for m in (2, 3)]
@@ -102,31 +106,40 @@ def tile_picked_deform_lin_none_def_e_kernel(tc, xT, w, offs, out):
                 )
                 done[bank] += 1
 
-        def round_shared(g, cut):
-            round_scalar(w_rounded[g][:, cut:, :], w_raw[g][:, :, cut:])
-            round_vector(w_rounded[g][:, 0:cut, :], w_raw[g][:, :, 0:cut])
+        def round_load(first, raw, cut):
+            count = raw.shape[1]
+            for i in range(count):
+                round_scalar(w_rounded[first + i][:, cut:, :], raw[:, i, :, cut:])
+            nc.vector.tensor_copy(
+                out=all_rounded[:, first : first + count, 0:cut, :].rearrange("p g (c i) j -> p g c j i", i=2),
+                in_=raw[:, :, :, 0:cut].rearrange("p g j (c i) -> p g c j i", i=2),
+            )
 
-        for g in (0, 1, 2):
-            round_shared(g, half)
-        for g in (0, 1, 2):
-            quantize_w(g, 0, M)
-        for g in (3, 4):
-            round_shared(g, 288)
+        round_load(0, w_loads[0], half)
+        quantize(
+            all_codes[:, 0:2].rearrange("p g c -> p (g c)"),
+            all_scales[:, 0:2].rearrange("p g c -> p (g c)"),
+            all_rounded[:, 0:2].rearrange("p g c j -> p (g c) j"),
+        )
+        quantize_w(2, 0, M)
+        round_load(3, w_loads[1], 288)
         for g in (3, 4):
             quantize_w(g, 0, M)
         for g in (3, 0, 4, 1):
             multiply(g, range(4))
 
-        for g in (5, 6):
-            round_scalar(w_rounded[g][:, half:, :], w_raw[g][:, :, half:])
-            for m in (0, 1):
-                round_vector(w_rounded[g][:, m * BLOCK : (m + 1) * BLOCK, :], w_raw[g][:, :, m * BLOCK : (m + 1) * BLOCK])
-            for m in (0, 1):
-                quantize_w(g, m * BLOCK, (m + 1) * BLOCK)
-            multiply(g, (0, 1))
-            if g == 5:
-                quantize_w(g, half, M)
-                multiply(g, (2, 3))
+        round_scalar(w_rounded[5][:, half:, :], w_raw[5][:, :, half:])
+        round_vector(w_rounded[5][:, 0:half, :], w_raw[5][:, :, 0:half])
+        for lo in (0, half):
+            quantize_w(5, lo, lo + half)
+            multiply(5, (lo // BLOCK, lo // BLOCK + 1))
+
+        round_scalar(w_rounded[6][:, half:, :], w_raw[6][:, :, half:])
+        for m in (0, 1):
+            round_vector(w_rounded[6][:, m * BLOCK : (m + 1) * BLOCK, :], w_raw[6][:, :, m * BLOCK : (m + 1) * BLOCK])
+        for m in (0, 1):
+            quantize_w(6, m * BLOCK, (m + 1) * BLOCK)
+        multiply(6, (0, 1))
         multiply(2, (0, 1))
 
         last = w_rounded[7]

@@ -144,17 +144,18 @@ def tile_picked_deform_lin_none_def_e_kernel(tc, xT, w, offs, out):
 
         last = w_rounded[7]
         round_vector(last[:, 0:128, :], low_raw[:, :, 0:128])
-        round_scalar(last[:, 128:256, :], low_raw[:, :, 128:256])
+        round_vector(last[:, 128:160, :], low_raw[:, :, 128:160])
+        round_scalar(last[:, 160:256, :], low_raw[:, :, 160:256])
         quantize_w(6, half, M)
         multiply(6, (2, 3))
         multiply(2, (2, 3))
         for m in (0, 1):
             quantize_w(7, m * BLOCK, (m + 1) * BLOCK)
             multiply(7, (m,))
-        round_scalar(last[:, 256:336, :], high_raw[:, :, 0:80])
+        round_scalar(last[:, 256:320, :], high_raw[:, :, 0:64])
         for lo in (128, 192):
             round_vector(last[:, half + lo : half + lo + 64, :], high_raw[:, :, lo : lo + 64])
-        round_vector(last[:, 336:384, :], high_raw[:, :, 80:128])
+        round_vector(last[:, 320:384, :], high_raw[:, :, 64:128])
 
         first_pair = shared[:, 0 : 2 * V].rearrange("p (m v) -> p m v", m=2)
         nc.scalar.copy(out=first_pair, in_=pair[:])
@@ -162,7 +163,8 @@ def tile_picked_deform_lin_none_def_e_kernel(tc, xT, w, offs, out):
         for lo in (384, 448):
             quantize_w(7, lo, lo + 64)
         multiply(7, (3,))
-        quantize_w(7, 256, 384)
+        for lo in (256, 320):
+            quantize_w(7, lo, lo + 64)
         multiply(7, (2,))
         for m, engine_copy in ((3, nc.scalar.copy), (2, nc.vector.tensor_copy)):
             result = keep.tile([BLOCK, V], F32, name=f"result{m}", align_bytes=DMA_ALIGN)

@@ -39,7 +39,7 @@ def tile_picked_deform_lin_none_def_e_kernel(tc, xT, w, offs, out):
     with tc.tile_pool(name="keep", bufs=1) as keep, tc.psum_pool(name="psum", bufs=1) as psum:
         offsets = keep.tile([P, S // 16], U16, name="offsets", align_bytes=DMA_ALIGN)
         x_passes = xT.rearrange("(a p j) t -> a p j t", a=PASSES, j=PACK)
-        x_raw = [keep.tile([P, PACK, T], F32, name=f"x_raw{a}", align_bytes=DMA_ALIGN) for a in range(PASSES)]
+        x_raw = [keep.tile([P, PACK, T], F32, name=f"x_raw{a}", tag=f"x_raw{a}", align_bytes=DMA_ALIGN) for a in range(PASSES)]
         nc.sync.dma_start(out=x_raw[0][:], in_=x_passes[0])
         nc.sync.dma_start(offsets[:], offs)
         nc.sync.dma_start(out=x_raw[1][:], in_=x_passes[1])
@@ -52,11 +52,8 @@ def tile_picked_deform_lin_none_def_e_kernel(tc, xT, w, offs, out):
             w_raw.extend(raw[:, i] for i in range(count))
             w_loads.append(raw)
         half = M // 2
-        low_raw = keep.tile([P, PACK, half], F32, name="low_raw", align_bytes=DMA_ALIGN)
-        nc.sync.dma_start(out=low_raw[:], in_=w_passes[:, 7, :, 0:half])
-        shared = keep.tile([P, 192 + PACK * half], F32, name="high_raw", align_bytes=DMA_ALIGN)
-        high_raw = shared[:, 192:].rearrange("p (j c) -> p j c", j=PACK)
-        nc.sync.dma_start(out=high_raw, in_=w_passes[:, 7, :, half:M])
+        shared = w_raw[0].rearrange("p j c -> p (j c)")
+        high_raw = shared[:, 192 : 192 + PACK * half].rearrange("p (j c) -> p j c", j=PACK)
 
         x_scales = keep.tile([P, T], U8, name="x_scales", align_bytes=ALIGN)
         nc.gpsimd.memset(x_scales[:], 0)
@@ -74,6 +71,8 @@ def tile_picked_deform_lin_none_def_e_kernel(tc, xT, w, offs, out):
                 quantize(x_codes[a][:, c0 : c0 + width], x_scales[4 * a : P, c0 : c0 + width], rounded[:, c0 : c0 + width, :])
             nc.vector.tensor_copy(picked_codes[a][:], x_codes[a][:].indirect(offsets[:]))
         nc.vector.tensor_copy(picked_scales[:], x_scales[:].indirect(offsets[:]))
+        low_raw = keep.tile([P, PACK, half], F32, name="low_raw", tag="x_raw1", align_bytes=DMA_ALIGN)
+        nc.sync.dma_start(out=low_raw[:], in_=w_passes[:, 7, :, 0:half])
 
         all_codes = keep.tile([P, D * PASSES, M], U32, name="w_codes", align_bytes=ALIGN)
         all_scales = keep.tile([P, D * PASSES, M], U8, name="w_scales", align_bytes=ALIGN)
@@ -116,6 +115,7 @@ def tile_picked_deform_lin_none_def_e_kernel(tc, xT, w, offs, out):
             )
 
         round_load(0, w_loads[0], half)
+        nc.sync.dma_start(out=high_raw, in_=w_passes[:, 7, :, half:M])
         quantize(
             all_codes[:, 0:2].rearrange("p g c -> p (g c)"),
             all_scales[:, 0:2].rearrange("p g c -> p (g c)"),

@@ -166,7 +166,7 @@ def tile_picked_deform_lin_none_def_e_kernel(tc, xT, w, offs, out):
         for lo in (256, 320):
             quantize_w(7, lo, lo + 64)
         multiply(7, (2,))
-        for m, engine_copy in ((3, nc.scalar.copy), (2, nc.vector.tensor_copy)):
+        for m, engine_copy in ((3, nc.vector.tensor_copy), (2, nc.vector.tensor_copy)):
             result = keep.tile([BLOCK, V], F32, name=f"result{m}", align_bytes=DMA_ALIGN)
             engine_copy(out=result[:], in_=acc[m])
             nc.sync.dma_start(out=out[m * BLOCK : (m + 1) * BLOCK, :], in_=result[:])

@@ -125,7 +125,7 @@ def tile_picked_deform_lin_none_def_e_kernel(tc, xT, w, offs, out):
         round_load(3, w_loads[1], 288)
         for g in (3, 4):
             quantize_w(g, 0, M)
-        for g in (3, 0, 4, 1):
+        for g in (3, 4):
             multiply(g, range(4))
 
         round_scalar(w_rounded[5][:, half:, :], w_raw[5][:, :, half:])
@@ -133,6 +133,8 @@ def tile_picked_deform_lin_none_def_e_kernel(tc, xT, w, offs, out):
         for lo in (0, half):
             quantize_w(5, lo, lo + half)
             multiply(5, (lo // BLOCK, lo // BLOCK + 1))
+        for g in range(3):
+            multiply(g, (2, 3))
 
         round_scalar(w_rounded[6][:, half:, :], w_raw[6][:, :, half:])
         for m in (0, 1):
@@ -140,7 +142,8 @@ def tile_picked_deform_lin_none_def_e_kernel(tc, xT, w, offs, out):
         for m in (0, 1):
             quantize_w(6, m * BLOCK, (m + 1) * BLOCK)
         multiply(6, (0, 1))
-        multiply(2, (0, 1))
+        for g in range(3):
+            multiply(g, (0, 1))
 
         last = w_rounded[7]
         round_vector(last[:, 0:128, :], low_raw[:, :, 0:128])
@@ -148,7 +151,6 @@ def tile_picked_deform_lin_none_def_e_kernel(tc, xT, w, offs, out):
         round_scalar(last[:, 160:256, :], low_raw[:, :, 160:256])
         quantize_w(6, half, M)
         multiply(6, (2, 3))
-        multiply(2, (2, 3))
         for m in (0, 1):
             quantize_w(7, m * BLOCK, (m + 1) * BLOCK)
             multiply(7, (m,))

@@ -23,7 +23,10 @@ def tile_picked_deform_lin_none_def_e_kernel(tc, xT, w, offs, out):
     nc = tc.nc
 
     def views(rounded, raw):
-        return rounded.rearrange("p (c i) j -> p c j i", i=2), raw.rearrange("p j (c i) -> p c j i", i=2)
+        return (
+            rounded.rearrange("p (c i) (u e) -> p c u i e", i=4, e=2),
+            raw.rearrange("p (u e) (c i) -> p c u i e", i=4, e=2),
+        )
 
     def round_vector(rounded, raw):
         dst, src = views(rounded, raw)

@@ -112,10 +112,8 @@ def tile_picked_deform_lin_none_def_e_kernel(tc, xT, w, offs, out):
             count = raw.shape[1]
             for i in range(count):
                 round_scalar(w_rounded[first + i][:, cut:, :], raw[:, i, :, cut:])
-            nc.vector.tensor_copy(
-                out=all_rounded[:, first : first + count, 0:cut, :].rearrange("p g (c i) j -> p g c j i", i=2),
-                in_=raw[:, :, :, 0:cut].rearrange("p g j (c i) -> p g c j i", i=2),
-            )
+            for i in range(count):
+                round_vector(w_rounded[first + i][:, 0:cut, :], raw[:, i, :, 0:cut])
 
         round_load(0, w_loads[0], half)
         nc.sync.dma_start(out=high_raw, in_=w_passes[:, 7, :, half:M])

@@ -9,12 +9,14 @@ U32 = mybir.dt.uint32
 U16 = mybir.dt.uint16
 U8 = mybir.dt.uint8
 FP8X4 = mybir.dt.float8_e4m3fn_x4
+COPY = mybir.ActivationFunctionType.Copy
 
 P = 128
 PACK = 4
 PASSES = K // (P * PACK)
 BLOCK = 128
-CHUNK = 512
+HALF = M // 2
+TAP = V // 16
 ALIGN = 64
 DMA_ALIGN = 256
 
@@ -41,41 +43,51 @@ def tile_picked_deform_lin_none_def_e_kernel(tc, xT, w, offs, out):
 
     with tc.tile_pool(name="keep", bufs=1) as keep, tc.psum_pool(name="psum", bufs=1) as psum:
         offsets = keep.tile([P, S // 16], U16, name="offsets", align_bytes=DMA_ALIGN)
-        x_passes = xT.rearrange("(a p j) t -> a p j t", a=PASSES, j=PACK)
-        x_raw = [keep.tile([P, PACK, T], F32, name=f"x_raw{a}", tag=f"x_raw{a}", align_bytes=DMA_ALIGN) for a in range(PASSES)]
-        nc.sync.dma_start(out=x_raw[0][:], in_=x_passes[0])
+        x_raw = keep.tile([P, PASSES, PACK, T], F32, name="x_raw", align_bytes=DMA_ALIGN)
+        nc.sync.dma_start(out=x_raw[:], in_=xT.rearrange("(a p j) t -> p a j t", a=PASSES, j=PACK))
         nc.sync.dma_start(offsets[:], offs)
-        nc.sync.dma_start(out=x_raw[1][:], in_=x_passes[1])
+
+        constant = keep.tile([P, 8], F32, name="constant")
+        unread = keep.tile([P, 8], F32, name="unread")
+        nc.gpsimd.memset(constant[:], 0.0)
+        nc.scalar.activation(unread[:], constant[:], COPY)
 
         w_passes = w.rearrange("d (a p j) m -> p (d a) j m", a=PASSES, j=PACK)
-        w_raw, w_loads = [], []
+        w_raw = []
         for first, count in ((0, 3), (3, 2), (5, 1), (6, 1)):
             raw = keep.tile([P, count, PACK, M], F32, name=f"w_raw{first}", align_bytes=DMA_ALIGN)
             nc.sync.dma_start(out=raw[:], in_=w_passes[:, first : first + count])
             w_raw.extend(raw[:, i] for i in range(count))
-            w_loads.append(raw)
-        half = M // 2
-        shared = w_raw[0].rearrange("p j c -> p (j c)")
-        high_raw = shared[:, 192 : 192 + PACK * half].rearrange("p (j c) -> p j c", j=PACK)
 
-        x_scales = keep.tile([P, T], U8, name="x_scales", align_bytes=ALIGN)
-        nc.gpsimd.memset(x_scales[:], 0)
-        x_codes = [keep.tile([P, T], U32, name=f"x_codes{a}", align_bytes=ALIGN) for a in range(PASSES)]
-        picked_codes = [keep.tile([P, S], U32, name=f"picked_codes{a}", align_bytes=ALIGN) for a in range(PASSES)]
-        picked_scales = keep.tile([P, S], U8, name="picked_scales", align_bytes=ALIGN)
+        def reuse(g, width):
+            return w_raw[g].rearrange("p j c -> p (j c)")[:, 0 : PACK * width].rearrange("p (j c) -> p j c", j=PACK)
 
-        vector_share_of_x = 576
-        for a in range(PASSES):
-            rounded = keep.tile([P, T, PACK], BF16, name=f"rounded_x{a}", align_bytes=ALIGN)
-            round_scalar(rounded[:, vector_share_of_x:, :], x_raw[a][:, :, vector_share_of_x:])
-            round_vector(rounded[:, 0:vector_share_of_x, :], x_raw[a][:, :, 0:vector_share_of_x])
-            width = T if a == 0 else CHUNK
-            for c0 in range(0, T, width):
-                quantize(x_codes[a][:, c0 : c0 + width], x_scales[4 * a : P, c0 : c0 + width], rounded[:, c0 : c0 + width, :])
-            nc.vector.tensor_copy(picked_codes[a][:], x_codes[a][:].indirect(offsets[:]))
-        nc.vector.tensor_copy(picked_scales[:], x_scales[:].indirect(offsets[:]))
-        low_raw = keep.tile([P, PACK, half], F32, name="low_raw", tag="x_raw1", align_bytes=DMA_ALIGN)
-        nc.sync.dma_start(out=low_raw[:], in_=w_passes[:, 7, :, 0:half])
+        low_raw, third_raw, last_raw = reuse(0, HALF), reuse(3, BLOCK), reuse(4, BLOCK)
+
+        picked = [keep.tile([P, PACK, S], F32, name=f"picked{a}", align_bytes=ALIGN) for a in range(PASSES)]
+        x_rounded = [keep.tile([P, S, PACK], BF16, name=f"x_rounded{a}", align_bytes=ALIGN) for a in range(PASSES)]
+        x_codes = [keep.tile([P, S], U32, name=f"x_codes{a}", align_bytes=ALIGN) for a in range(PASSES)]
+        x_scales = [keep.tile([P, S], U8, name=f"x_scales{a}", align_bytes=ALIGN) for a in range(PASSES)]
+
+        for a, d in [(0, 3)] + [(1, d) for d in range(D)]:
+            for j in range(PACK):
+                nc.scalar.activation(picked[a][:, j, d * V : (d + 1) * V], x_raw[:, a, j, :].indirect(offsets[:, d * TAP : (d + 1) * TAP]), COPY)
+        for j in range(PACK):
+            nc.vector.tensor_copy(picked[0][:, j, 0 : 3 * V], x_raw[:, 0, j, :].indirect(offsets[:, 0 : 3 * TAP]))
+
+        def round_x(a, lo, hi):
+            round_vector(x_rounded[a][:, lo:hi, :], picked[a][:, :, lo:hi])
+
+        def quantize_x(a, lo, hi):
+            quantize(x_codes[a][:, lo:hi], x_scales[a][:, lo:hi], x_rounded[a][:, lo:hi, :])
+
+        x_late = w_raw[0][:, 2, :].bitcast(BF16).rearrange("p (c j) -> p c j", j=PACK)
+
+        round_x(0, 3 * V, S)
+        round_x(1, 0, 2 * V)
+        round_x(0, 0, 3 * V)
+        quantize_x(1, 0, 2 * V)
+        quantize_x(0, 0, S)
 
         all_codes = keep.tile([P, D * PASSES, M], U32, name="w_codes", align_bytes=ALIGN)
         all_scales = keep.tile([P, D * PASSES, M], U8, name="w_scales", align_bytes=ALIGN)
@@ -101,75 +113,77 @@ def tile_picked_deform_lin_none_def_e_kernel(tc, xT, w, offs, out):
                     out=acc[m],
                     lhsT=w_codes[g][:, m * BLOCK : (m + 1) * BLOCK].bitcast(FP8X4),
                     lhsT_scale=w_scales[g][:, m * BLOCK : (m + 1) * BLOCK],
-                    rhs=picked_codes[a][:, d * V : (d + 1) * V].bitcast(FP8X4),
-                    rhs_scale=picked_scales[4 * a : P, d * V : (d + 1) * V],
+                    rhs=x_codes[a][:, d * V : (d + 1) * V].bitcast(FP8X4),
+                    rhs_scale=x_scales[a][:, d * V : (d + 1) * V],
                     start=(done[bank] == 0),
                     stop=(done[bank] == passes_of_bank[bank] - 1),
                 )
                 done[bank] += 1
 
-        def round_load(first, raw, cut):
-            count = raw.shape[1]
-            for i in range(count):
-                round_scalar(w_rounded[first + i][:, cut:, :], raw[:, i, :, cut:])
-            for i in range(count):
-                round_vector(w_rounded[first + i][:, 0:cut, :], raw[:, i, :, 0:cut])
+        def round_passes(passes, cut):
+            for g in passes:
+                round_scalar(w_rounded[g][:, cut:, :], w_raw[g][:, :, cut:])
+            for g in passes:
+                round_vector(w_rounded[g][:, 0:cut, :], w_raw[g][:, :, 0:cut])
 
-        round_load(0, w_loads[0], half)
-        nc.sync.dma_start(out=high_raw, in_=w_passes[:, 7, :, half:M])
-        quantize(
-            all_codes[:, 0:2].rearrange("p g c -> p (g c)"),
-            all_scales[:, 0:2].rearrange("p g c -> p (g c)"),
-            all_rounded[:, 0:2].rearrange("p g c j -> p (g c) j"),
-        )
-        quantize_w(2, 0, M)
-        round_load(3, w_loads[1], 288)
+        round_vector(w_rounded[0], w_raw[0])
+        round_scalar(w_rounded[1], w_raw[1])
+        round_vector(x_late, picked[1][:, :, 2 * V : S])
+        nc.sync.dma_start(out=low_raw, in_=w_passes[:, 7, :, 0:HALF])
+        round_vector(w_rounded[2][:, 0:HALF, :], w_raw[2][:, :, 0:HALF])
+        round_scalar(w_rounded[2][:, HALF:, :], w_raw[2][:, :, HALF:])
+        quantize_w(0, 0, M)
+        quantize(x_codes[1][:, 2 * V : S], x_scales[1][:, 2 * V : S], x_late)
+        quantize_w(2, 0, HALF)
+        quantize_w(1, 0, M)
+        quantize_w(2, HALF, M)
+        multiply(2, range(4))
+        round_passes((3, 4), 288)
+        nc.sync.dma_start(out=third_raw, in_=w_passes[:, 7, :, HALF : HALF + BLOCK])
+        nc.sync.dma_start(out=last_raw, in_=w_passes[:, 7, :, HALF + BLOCK : M])
         for g in (3, 4):
             quantize_w(g, 0, M)
         for g in (3, 4):
             multiply(g, range(4))
 
-        round_scalar(w_rounded[5][:, half:, :], w_raw[5][:, :, half:])
-        round_vector(w_rounded[5][:, 0:half, :], w_raw[5][:, :, 0:half])
-        for lo in (0, half):
-            quantize_w(5, lo, lo + half)
+        round_passes((5,), HALF)
+        for lo in (0, HALF):
+            quantize_w(5, lo, lo + HALF)
             multiply(5, (lo // BLOCK, lo // BLOCK + 1))
-        for g in range(3):
+        for g in (0, 1):
             multiply(g, (2, 3))
 
-        round_scalar(w_rounded[6][:, half:, :], w_raw[6][:, :, half:])
+        round_scalar(w_rounded[6][:, HALF:, :], w_raw[6][:, :, HALF:])
         for m in (0, 1):
             round_vector(w_rounded[6][:, m * BLOCK : (m + 1) * BLOCK, :], w_raw[6][:, :, m * BLOCK : (m + 1) * BLOCK])
         for m in (0, 1):
             quantize_w(6, m * BLOCK, (m + 1) * BLOCK)
         multiply(6, (0, 1))
-        for g in range(3):
+        for g in (0, 1):
             multiply(g, (0, 1))
 
         last = w_rounded[7]
         round_vector(last[:, 0:128, :], low_raw[:, :, 0:128])
         round_vector(last[:, 128:160, :], low_raw[:, :, 128:160])
         round_scalar(last[:, 160:256, :], low_raw[:, :, 160:256])
-        quantize_w(6, half, M)
+        quantize_w(6, HALF, M)
         multiply(6, (2, 3))
         for m in (0, 1):
             quantize_w(7, m * BLOCK, (m + 1) * BLOCK)
             multiply(7, (m,))
-        round_scalar(last[:, 256:320, :], high_raw[:, :, 0:64])
-        for lo in (128, 192):
-            round_vector(last[:, half + lo : half + lo + 64, :], high_raw[:, :, lo : lo + 64])
-        round_vector(last[:, 320:384, :], high_raw[:, :, 64:128])
-
-        first_pair = shared[:, 0 : 2 * V].rearrange("p (m v) -> p m v", m=2)
-        nc.scalar.copy(out=first_pair, in_=pair[:])
-        nc.sync.dma_start(out=out[0 : 2 * BLOCK, :].rearrange("(m p) v -> p m v", p=BLOCK), in_=first_pair)
+        round_scalar(last[:, 256:384, :], third_raw)
+        round_vector(last[:, 384:448, :], last_raw[:, :, 0:64])
+        round_vector(last[:, 448:512, :], last_raw[:, :, 64:128])
+        quantize_w(7, 256, 384)
+        multiply(7, (2,))
         for lo in (384, 448):
             quantize_w(7, lo, lo + 64)
         multiply(7, (3,))
-        for lo in (256, 320):
-            quantize_w(7, lo, lo + 64)
-        multiply(7, (2,))
-        for m, engine_copy in ((3, nc.vector.tensor_copy), (2, nc.vector.tensor_copy)):
+
+        first_pair = w_raw[3].rearrange("p j c -> p (j c)")[:, 448 : 448 + 2 * V].rearrange("p (m v) -> p m v", m=2)
+        nc.scalar.copy(out=first_pair, in_=pair[:])
+        nc.sync.dma_start(out=out[0 : 2 * BLOCK, :].rearrange("(m p) v -> p m v", p=BLOCK), in_=first_pair)
+        for m in (2, 3):
             result = keep.tile([BLOCK, V], F32, name=f"result{m}", align_bytes=DMA_ALIGN)
-            engine_copy(out=result[:], in_=acc[m])
+            nc.vector.tensor_copy(out=result[:], in_=acc[m])
             nc.sync.dma_start(out=out[m * BLOCK : (m + 1) * BLOCK, :], in_=result[:])

@@ -173,17 +173,18 @@ def tile_picked_deform_lin_none_def_e_kernel(tc, xT, w, offs, out):
             multiply(7, (m,))
         round_scalar(last[:, 256:384, :], third_raw)
         round_vector(last[:, 384:448, :], last_raw[:, :, 0:64])
-        round_vector(last[:, 448:512, :], last_raw[:, :, 64:128])
+        round_vector(last[:, 448:480, :], last_raw[:, :, 64:96])
+        round_scalar(last[:, 480:512, :], last_raw[:, :, 96:128])
         quantize_w(7, 256, 384)
         multiply(7, (2,))
         for lo in (384, 448):
             quantize_w(7, lo, lo + 64)
         multiply(7, (3,))
 
-        first_pair = w_raw[3].rearrange("p j c -> p (j c)")[:, 448 : 448 + 2 * V].rearrange("p (m v) -> p m v", m=2)
+        first_pair = w_raw[4].rearrange("p j c -> p (j c)")[:, 448 : 448 + 2 * V].rearrange("p (m v) -> p m v", m=2)
         nc.scalar.copy(out=first_pair, in_=pair[:])
         nc.sync.dma_start(out=out[0 : 2 * BLOCK, :].rearrange("(m p) v -> p m v", p=BLOCK), in_=first_pair)
-        for m in (2, 3):
+        for m, empty in ((2, nc.scalar.copy), (3, nc.vector.tensor_copy)):
             result = keep.tile([BLOCK, V], F32, name=f"result{m}", align_bytes=DMA_ALIGN)
-            nc.vector.tensor_copy(out=result[:], in_=acc[m])
+            empty(out=result[:], in_=acc[m])
             nc.sync.dma_start(out=out[m * BLOCK : (m + 1) * BLOCK, :], in_=result[:])

@@ -130,15 +130,14 @@ def tile_picked_deform_lin_none_def_e_kernel(tc, xT, w, offs, out):
         round_scalar(w_rounded[1], w_raw[1])
         round_vector(x_late, picked[1][:, :, 2 * V : S])
         nc.sync.dma_start(out=low_raw, in_=w_passes[:, 7, :, 0:HALF])
-        round_vector(w_rounded[2][:, 0:HALF, :], w_raw[2][:, :, 0:HALF])
-        round_scalar(w_rounded[2][:, HALF:, :], w_raw[2][:, :, HALF:])
+        round_vector(w_rounded[2][:, 0:320, :], w_raw[2][:, :, 0:320])
+        round_scalar(w_rounded[2][:, 320:, :], w_raw[2][:, :, 320:])
         quantize_w(0, 0, M)
         quantize(x_codes[1][:, 2 * V : S], x_scales[1][:, 2 * V : S], x_late)
         quantize_w(2, 0, HALF)
         quantize_w(1, 0, M)
         quantize_w(2, HALF, M)
-        multiply(2, range(4))
-        round_passes((3, 4), 288)
+        round_passes((3, 4), 320)
         nc.sync.dma_start(out=third_raw, in_=w_passes[:, 7, :, HALF : HALF + BLOCK])
         nc.sync.dma_start(out=last_raw, in_=w_passes[:, 7, :, HALF + BLOCK : M])
         for g in (3, 4):
@@ -146,11 +145,11 @@ def tile_picked_deform_lin_none_def_e_kernel(tc, xT, w, offs, out):
         for g in (3, 4):
             multiply(g, range(4))
 
-        round_passes((5,), HALF)
+        round_passes((5,), 288)
         for lo in (0, HALF):
             quantize_w(5, lo, lo + HALF)
             multiply(5, (lo // BLOCK, lo // BLOCK + 1))
-        for g in (0, 1):
+        for g in range(3):
             multiply(g, (2, 3))
 
         round_scalar(w_rounded[6][:, HALF:, :], w_raw[6][:, :, HALF:])
@@ -159,7 +158,7 @@ def tile_picked_deform_lin_none_def_e_kernel(tc, xT, w, offs, out):
         for m in (0, 1):
             quantize_w(6, m * BLOCK, (m + 1) * BLOCK)
         multiply(6, (0, 1))
-        for g in (0, 1):
+        for g in range(3):
             multiply(g, (0, 1))
 
         last = w_rounded[7]

@@ -163,8 +163,7 @@ def tile_picked_deform_lin_none_def_e_kernel(tc, xT, w, offs, out):
 
         last = w_rounded[7]
         round_vector(last[:, 0:128, :], low_raw[:, :, 0:128])
-        round_vector(last[:, 128:160, :], low_raw[:, :, 128:160])
-        round_scalar(last[:, 160:256, :], low_raw[:, :, 160:256])
+        round_scalar(last[:, 128:256, :], low_raw[:, :, 128:256])
         quantize_w(6, HALF, M)
         multiply(6, (2, 3))
         for m in (0, 1):

@@ -126,7 +126,8 @@ def tile_picked_deform_lin_none_def_e_kernel(tc, xT, w, offs, out):
             for g in passes:
                 round_vector(w_rounded[g][:, 0:cut, :], w_raw[g][:, :, 0:cut])
 
-        round_vector(w_rounded[0], w_raw[0])
+        for lo in (0, HALF):
+            round_vector(w_rounded[0][:, lo : lo + HALF, :], w_raw[0][:, :, lo : lo + HALF])
         round_scalar(w_rounded[1], w_raw[1])
         round_vector(x_late, picked[1][:, :, 2 * V : S])
         nc.sync.dma_start(out=low_raw, in_=w_passes[:, 7, :, 0:HALF])
@@ -135,7 +136,8 @@ def tile_picked_deform_lin_none_def_e_kernel(tc, xT, w, offs, out):
         quantize_w(0, 0, M)
         quantize(x_codes[1][:, 2 * V : S], x_scales[1][:, 2 * V : S], x_late)
         quantize_w(2, 0, HALF)
-        quantize_w(1, 0, M)
+        for lo in (0, HALF):
+            quantize_w(1, lo, lo + HALF)
         quantize_w(2, HALF, M)
         round_passes((3, 4), 320)
         nc.sync.dma_start(out=third_raw, in_=w_passes[:, 7, :, HALF : HALF + BLOCK])

@@ -85,7 +85,8 @@ def tile_picked_deform_lin_none_def_e_kernel(tc, xT, w, offs, out):
 
         round_x(0, 3 * V, S)
         round_x(1, 0, 2 * V)
-        round_x(0, 0, 3 * V)
+        for d in range(3):
+            round_x(0, d * V, (d + 1) * V)
         quantize_x(1, 0, 2 * V)
         quantize_x(0, 0, S)
 
@@ -173,11 +174,10 @@ def tile_picked_deform_lin_none_def_e_kernel(tc, xT, w, offs, out):
             multiply(7, (m,))
         round_scalar(last[:, 256:384, :], third_raw)
         round_vector(last[:, 384:448, :], last_raw[:, :, 0:64])
-        round_vector(last[:, 448:480, :], last_raw[:, :, 64:96])
-        round_scalar(last[:, 480:512, :], last_raw[:, :, 96:128])
+        round_scalar(last[:, 448:512, :], last_raw[:, :, 64:128])
         quantize_w(7, 256, 384)
         multiply(7, (2,))
-        for lo in (384, 448):
+        for lo in (448, 384):
             quantize_w(7, lo, lo + 64)
         multiply(7, (3,))
 

@@ -85,8 +85,7 @@ def tile_picked_deform_lin_none_def_e_kernel(tc, xT, w, offs, out):
 
         round_x(0, 3 * V, S)
         round_x(1, 0, 2 * V)
-        for d in range(3):
-            round_x(0, d * V, (d + 1) * V)
+        round_x(0, 0, 3 * V)
         quantize_x(1, 0, 2 * V)
         quantize_x(0, 0, S)
 
@@ -172,7 +171,8 @@ def tile_picked_deform_lin_none_def_e_kernel(tc, xT, w, offs, out):
         for m in (0, 1):
             quantize_w(7, m * BLOCK, (m + 1) * BLOCK)
             multiply(7, (m,))
-        round_scalar(last[:, 256:384, :], third_raw)
+        round_scalar(last[:, 256:352, :], third_raw[:, :, 0:96])
+        round_vector(last[:, 352:384, :], third_raw[:, :, 96:128])
         round_vector(last[:, 384:448, :], last_raw[:, :, 0:64])
         round_scalar(last[:, 448:512, :], last_raw[:, :, 64:128])
         quantize_w(7, 256, 384)

import concourse.mybir as mybir

D, K, T, S, V, M = 4, 1024, 1024, 512, 128, 512
FLOPS = 2 * K * M * S

F32 = mybir.dt.float32
BF16 = mybir.dt.bfloat16
U32 = mybir.dt.uint32
U16 = mybir.dt.uint16
U8 = mybir.dt.uint8
FP8X4 = mybir.dt.float8_e4m3fn_x4
COPY = mybir.ActivationFunctionType.Copy

P = 128
PACK = 4
PASSES = K // (P * PACK)
BLOCK = 128
HALF = M // 2
TAP = V // 16
ALIGN = 64
DMA_ALIGN = 256


def tile_picked_deform_lin_none_def_e_kernel(tc, xT, w, offs, out):
    nc = tc.nc

    def views(rounded, raw):
        return (
            rounded.rearrange("p (c i) (u e) -> p c u i e", i=4, e=2),
            raw.rearrange("p (u e) (c i) -> p c u i e", i=4, e=2),
        )

    def round_vector(rounded, raw):
        dst, src = views(rounded, raw)
        nc.vector.tensor_copy(out=dst, in_=src)

    def round_scalar(rounded, raw):
        dst, src = views(rounded, raw)
        nc.scalar.copy(out=dst, in_=src)

    def quantize(codes, scales, rounded):
        nc.vector.quantize_mx(out=codes.bitcast(FP8X4), scales=scales, in_=rounded.rearrange("p c j -> p (c j)"))

    with tc.tile_pool(name="keep", bufs=1) as keep, tc.psum_pool(name="psum", bufs=1) as psum:
        offsets = keep.tile([P, S // 16], U16, name="offsets", align_bytes=DMA_ALIGN)
        x_raw = keep.tile([P, PASSES, PACK, T], F32, name="x_raw", align_bytes=DMA_ALIGN)
        nc.sync.dma_start(out=x_raw[:], in_=xT.rearrange("(a p j) t -> p a j t", a=PASSES, j=PACK))
        nc.sync.dma_start(offsets[:], offs)

        constant = keep.tile([P, 8], F32, name="constant")
        unread = keep.tile([P, 8], F32, name="unread")
        nc.gpsimd.memset(constant[:], 0.0)
        nc.scalar.activation(unread[:], constant[:], COPY)

        w_passes = w.rearrange("d (a p j) m -> p (d a) j m", a=PASSES, j=PACK)
        w_raw = []
        for first, count in ((0, 3), (3, 2), (5, 1), (6, 1)):
            raw = keep.tile([P, count, PACK, M], F32, name=f"w_raw{first}", align_bytes=DMA_ALIGN)
            nc.sync.dma_start(out=raw[:], in_=w_passes[:, first : first + count])
            w_raw.extend(raw[:, i] for i in range(count))

        def reuse(g, width):
            return w_raw[g].rearrange("p j c -> p (j c)")[:, 0 : PACK * width].rearrange("p (j c) -> p j c", j=PACK)

        low_raw, third_raw, last_raw = reuse(0, HALF), reuse(3, BLOCK), reuse(4, BLOCK)

        picked = [keep.tile([P, PACK, S], F32, name=f"picked{a}", align_bytes=ALIGN) for a in range(PASSES)]
        x_rounded = [keep.tile([P, S, PACK], BF16, name=f"x_rounded{a}", align_bytes=ALIGN) for a in range(PASSES)]
        x_codes = [keep.tile([P, S], U32, name=f"x_codes{a}", align_bytes=ALIGN) for a in range(PASSES)]
        x_scales = [keep.tile([P, S], U8, name=f"x_scales{a}", align_bytes=ALIGN) for a in range(PASSES)]

        for a, d in [(0, 3)] + [(1, d) for d in range(D)]:
            for j in range(PACK):
                nc.scalar.activation(picked[a][:, j, d * V : (d + 1) * V], x_raw[:, a, j, :].indirect(offsets[:, d * TAP : (d + 1) * TAP]), COPY)
        for j in range(PACK):
            nc.vector.tensor_copy(picked[0][:, j, 0 : 3 * V], x_raw[:, 0, j, :].indirect(offsets[:, 0 : 3 * TAP]))

        def round_x(a, lo, hi):
            round_vector(x_rounded[a][:, lo:hi, :], picked[a][:, :, lo:hi])

        def quantize_x(a, lo, hi):
            quantize(x_codes[a][:, lo:hi], x_scales[a][:, lo:hi], x_rounded[a][:, lo:hi, :])

        x_late = w_raw[0][:, 2, :].bitcast(BF16).rearrange("p (c j) -> p c j", j=PACK)

        round_x(0, 3 * V, S)
        round_x(1, 0, 2 * V)
        round_x(0, 0, 3 * V)
        quantize_x(1, 0, 2 * V)
        quantize_x(0, 0, S)

        all_codes = keep.tile([P, D * PASSES, M], U32, name="w_codes", align_bytes=ALIGN)
        all_scales = keep.tile([P, D * PASSES, M], U8, name="w_scales", align_bytes=ALIGN)
        all_rounded = keep.tile([P, D * PASSES, M, PACK], BF16, name="w_rounded", align_bytes=ALIGN)
        w_codes = [all_codes[:, g] for g in range(D * PASSES)]
        w_scales = [all_scales[:, g] for g in range(D * PASSES)]
        w_rounded = [all_rounded[:, g] for g in range(D * PASSES)]

        pair = psum.tile([BLOCK, 2, V], F32, name="pair")
        acc = [pair[:, 0, :], pair[:, 1, :]] + [psum.tile([BLOCK, V], F32, name=f"acc{m}")[:] for m in (2, 3)]
        bank_of = (0, 0, 1, 2)
        passes_of_bank = (2 * D * PASSES, D * PASSES, D * PASSES)
        done = [0, 0, 0]

        def quantize_w(g, c0, c1):
            quantize(w_codes[g][:, c0:c1], w_scales[g][:, c0:c1], w_rounded[g][:, c0:c1, :])

        def multiply(g, blocks):
            d, a = divmod(g, PASSES)
            for m in blocks:
                bank = bank_of[m]
                nc.tensor.matmul_mx(
                    out=acc[m],
                    lhsT=w_codes[g][:, m * BLOCK : (m + 1) * BLOCK].bitcast(FP8X4),
                    lhsT_scale=w_scales[g][:, m * BLOCK : (m + 1) * BLOCK],
                    rhs=x_codes[a][:, d * V : (d + 1) * V].bitcast(FP8X4),
                    rhs_scale=x_scales[a][:, d * V : (d + 1) * V],
                    start=(done[bank] == 0),
                    stop=(done[bank] == passes_of_bank[bank] - 1),
                )
                done[bank] += 1

        def round_passes(passes, cut):
            for g in passes:
                round_scalar(w_rounded[g][:, cut:, :], w_raw[g][:, :, cut:])
            for g in passes:
                round_vector(w_rounded[g][:, 0:cut, :], w_raw[g][:, :, 0:cut])

        for lo in (0, HALF):
            round_vector(w_rounded[0][:, lo : lo + HALF, :], w_raw[0][:, :, lo : lo + HALF])
        round_scalar(w_rounded[1], w_raw[1])
        round_vector(x_late, picked[1][:, :, 2 * V : S])
        nc.sync.dma_start(out=low_raw, in_=w_passes[:, 7, :, 0:HALF])
        round_vector(w_rounded[2][:, 0:320, :], w_raw[2][:, :, 0:320])
        round_scalar(w_rounded[2][:, 320:, :], w_raw[2][:, :, 320:])
        quantize_w(0, 0, M)
        quantize(x_codes[1][:, 2 * V : S], x_scales[1][:, 2 * V : S], x_late)
        quantize_w(2, 0, HALF)
        for lo in (0, HALF):
            quantize_w(1, lo, lo + HALF)
        quantize_w(2, HALF, M)
        round_passes((3, 4), 320)
        nc.sync.dma_start(out=third_raw, in_=w_passes[:, 7, :, HALF : HALF + BLOCK])
        nc.sync.dma_start(out=last_raw, in_=w_passes[:, 7, :, HALF + BLOCK : M])
        for g in (3, 4):
            quantize_w(g, 0, M)
        for g in (3, 4):
            multiply(g, range(4))

        round_passes((5,), 288)
        for lo in (0, HALF):
            quantize_w(5, lo, lo + HALF)
            multiply(5, (lo // BLOCK, lo // BLOCK + 1))
        for g in range(3):
            multiply(g, (2, 3))

        round_scalar(w_rounded[6][:, HALF:, :], w_raw[6][:, :, HALF:])
        for m in (0, 1):
            round_vector(w_rounded[6][:, m * BLOCK : (m + 1) * BLOCK, :], w_raw[6][:, :, m * BLOCK : (m + 1) * BLOCK])
        for m in (0, 1):
            quantize_w(6, m * BLOCK, (m + 1) * BLOCK)
        multiply(6, (0, 1))
        for g in range(3):
            multiply(g, (0, 1))

        last = w_rounded[7]
        round_vector(last[:, 0:128, :], low_raw[:, :, 0:128])
        round_scalar(last[:, 128:256, :], low_raw[:, :, 128:256])
        quantize_w(6, HALF, M)
        multiply(6, (2, 3))
        for m in (0, 1):
            quantize_w(7, m * BLOCK, (m + 1) * BLOCK)
            multiply(7, (m,))
        round_scalar(last[:, 256:352, :], third_raw[:, :, 0:96])
        round_vector(last[:, 352:384, :], third_raw[:, :, 96:128])
        round_vector(last[:, 384:448, :], last_raw[:, :, 0:64])
        round_scalar(last[:, 448:512, :], last_raw[:, :, 64:128])
        quantize_w(7, 256, 384)
        multiply(7, (2,))
        for lo in (448, 384):
            quantize_w(7, lo, lo + 64)
        multiply(7, (3,))

        first_pair = w_raw[4].rearrange("p j c -> p (j c)")[:, 448 : 448 + 2 * V].rearrange("p (m v) -> p m v", m=2)
        nc.scalar.copy(out=first_pair, in_=pair[:])
        nc.sync.dma_start(out=out[0 : 2 * BLOCK, :].rearrange("(m p) v -> p m v", p=BLOCK), in_=first_pair)
        for m, empty in ((2, nc.scalar.copy), (3, nc.vector.tensor_copy)):
            result = keep.tile([BLOCK, V], F32, name=f"result{m}", align_bytes=DMA_ALIGN)
            empty(out=result[:], in_=acc[m])
            nc.sync.dma_start(out=out[m * BLOCK : (m + 1) * BLOCK, :], in_=result[:])
